import numpy as np
import ml_dtypes


def mxq(x, axis, fmt="e4m3"):
    dtype, down = {"e4m3": (ml_dtypes.float8_e4m3fn, 7), "e5m2": (ml_dtypes.float8_e5m2, 14)}[fmt]
    v = np.moveaxis(np.asarray(x, np.float32).astype(ml_dtypes.bfloat16).astype(np.float64), axis, -1)
    blocks = v.reshape(v.shape[:-1] + (-1, 32))
    amax = np.abs(blocks).max(-1, keepdims=True)
    byte = np.maximum(np.where(amax > 0, np.frexp(amax)[1] - 1 + 127, 0) - down, 1)
    scale = np.exp2(byte - 127.0)
    codes = (blocks / scale).astype(np.float32).astype(dtype).astype(np.float64)
    return np.moveaxis((codes * scale).reshape(v.shape), -1, axis)


WIDE = False


def mx_kscale(k):
    if not WIDE:
        return np.ones(k)
    levels = np.array([10, -10, 5, -5, 0])
    if k % 512:
        return np.exp2(np.random.permutation(np.resize(levels, k // 32))).repeat(32)
    a = np.empty((k // 512, 16))
    for p in range(k // 512):
        a[p, :8] = np.random.permutation(np.resize(levels, 8))
        for g in range(8):
            far = levels[np.abs(levels - a[p, g]) >= 10]
            a[p, g + 8] = far[np.random.randint(len(far))]
    return np.exp2(a.ravel()).repeat(32)


def f64(x):
    return np.asarray(x).astype(np.float64)


def striped(idx):
    return np.tile(idx.reshape(-1, 16).T, (8, 1)).astype(np.uint16)


def unstriped(offs):
    return offs[:16].T.reshape(-1).astype(np.int64)


def pack_weight(w):
    k, n = w.shape
    w = f64(np.asarray(w, np.float32).astype(ml_dtypes.bfloat16)).reshape(k // 32, 32, n)
    amax = np.abs(w).max(1)
    byte = np.clip(np.where(amax > 0, np.frexp(amax)[1] - 1 + 127 - 7, 1), 1, 254)
    scaled = (w * np.exp2(127.0 - byte)[:, None, :]).reshape(k, n).astype(np.float32)
    words = np.ascontiguousarray(scaled.reshape(k // 512, 128, 4, n).transpose(0, 1, 3, 2)).astype(ml_dtypes.float8_e4m3fn).view(np.uint8)
    return words, np.ascontiguousarray(byte.astype(np.uint8).reshape(k // 512, 16, n))


def unpack_weight(words, scales):
    g, p, n, _ = words.shape
    vals = np.ascontiguousarray(words).view(ml_dtypes.float8_e4m3fn).astype(np.float64) * np.repeat(np.exp2(scales.astype(np.float64) - 127.0), 8, axis=1)[..., None]
    return vals.transpose(0, 1, 3, 2).reshape(g * 512, n)


def relu(v):
    return np.maximum(v, 0.0)


K, T, S, V, H, N = 512, 4096, 1024, 512, 512, 128


def setup_inputs():
    n = np.random.standard_normal
    s = mx_kscale(K)[:, None]
    u = mx_kscale(H)
    packed_xT = pack_weight(n((K, T)) * s)
    return {
        "x_words": packed_xT[0],
        "x_scales": packed_xT[1],
        "w1": (n((K, H)) / np.sqrt(K) / s * u).astype(np.float32),
        "w2": (n((H, N)) / np.sqrt(2 * H) / u[:, None]).astype(np.float32),
        "w3": (n((H, N)) / np.sqrt(2 * H) / u[:, None]).astype(np.float32),
        "offs": striped(np.random.permutation(T)[:S]),
        "cen": striped(np.random.permutation(S)[:V]),
        "pos1": striped(np.random.permutation(S)[:V]),
        "pos2": striped(np.random.permutation(S)[:V]),
        "pos3": striped(np.random.permutation(S)[:V]),
    }


def reference(x_words, x_scales, w1, w2, w3, offs, cen, pos1, pos2, pos3):
    xq = unpack_weight(x_words, x_scales)[:, unstriped(offs)]
    h = relu(mxq(f64(w1), 0, "e4m3").T @ xq)
    hc = h[:, unstriped(cen)]
    z = np.maximum(np.maximum(h[:, unstriped(pos1)], h[:, unstriped(pos2)]), h[:, unstriped(pos3)])
    return relu(mxq(f64(w2), 0, "e4m3").T @ mxq(hc, 0, "e4m3") + mxq(f64(w3), 0, "e4m3").T @ mxq(z, 0, "e4m3"))

@@ -1,0 +1,145 @@
+from contextlib import ExitStack
+
+import concourse.mybir as mybir
+
+K, T, S, V, H, N = 512, 4096, 1024, 512, 512, 128
+FLOPS = 2 * K * H * S + 2 * 2 * H * N * V
+
+F32 = mybir.dt.float32
+BF16 = mybir.dt.bfloat16
+I32 = mybir.dt.int32
+U32 = mybir.dt.uint32
+U16 = mybir.dt.uint16
+U8 = mybir.dt.uint8
+FP8X4 = mybir.dt.float8_e4m3fn_x4
+MAX = mybir.AluOpType.max
+RELU = mybir.ActivationFunctionType.Relu
+
+P = 128
+PACK = 4
+BANK = 512
+HEAD_COLS = 1024
+CHUNKS = ((0, 256), (256, 384), (384, 512))
+
+
+def tile_picked_sagecat_maxrelu_p_kernel(tc, x_words, x_scales, w1, w2, w3, offs, cen, pos1, pos2, pos3, out):
+    nc = tc.nc
+    with ExitStack() as ctx:
+        keep = ctx.enter_context(tc.tile_pool(name="keep", bufs=1))
+        psum = ctx.enter_context(tc.psum_pool(name="psum", bufs=1))
+
+        offs_sb = keep.tile([P, S // 16], U16, name="offs_sb")
+        cen_sb = keep.tile([P, V // 16], U16, name="cen_sb")
+        pos_sb = [keep.tile([P, V // 16], U16, name="pos_sb%d" % d) for d in range(3)]
+        table_words = keep.tile([P, T], I32, name="table_words", align_bytes=64)
+        table_scales = keep.tile([P, T], U8, name="table_scales", align_bytes=64)
+        w1_raw = keep.tile([P, PACK, H], F32, name="w1_raw", align_bytes=64)
+        w2_raw = keep.tile([P, PACK, N], F32, name="w2_raw", align_bytes=64)
+        w3_raw = keep.tile([P, PACK, N], F32, name="w3_raw", align_bytes=64)
+
+        nc.vector.memset(table_scales[:].bitcast(I32), 0)
+        words_hbm = x_words[0].rearrange("p c r -> p (c r)").bitcast(I32)
+        scales_hbm = x_scales[0].bitcast(I32)
+        nc.sync.dma_start(offs_sb[:], offs)
+        nc.sync.dma_start(table_words[:, :HEAD_COLS], words_hbm[:, :HEAD_COLS])
+        for q in range(4):
+            nc.sync.dma_start(table_scales[32 * q : 32 * q + 4, :].bitcast(I32), scales_hbm[4 * q : 4 * q + 4, :])
+        nc.sync.dma_start(table_words[:, HEAD_COLS:], words_hbm[:, HEAD_COLS:])
+        nc.sync.dma_start(w1_raw[:], w1.rearrange("(p j) c -> p j c", j=PACK))
+        for d, pos in enumerate((pos1, pos2, pos3)):
+            nc.sync.dma_start(pos_sb[d][:], pos)
+        nc.sync.dma_start(cen_sb[:], cen)
+        nc.sync.dma_start(w2_raw[:], w2.rearrange("(p j) c -> p j c", j=PACK))
+        nc.sync.dma_start(w3_raw[:], w3.rearrange("(p j) c -> p j c", j=PACK))
+
+        x_scale = keep.tile([P, S], U8, name="x_scale", align_bytes=64)
+        nc.vector.tensor_copy(x_scale[:], table_scales[:].indirect(offs_sb[:]))
+        x_codes = [keep.tile([P, BANK], U32, name="x_codes%d" % u, align_bytes=64) for u in range(2)]
+        for u in range(2):
+            nc.vector.tensor_copy(x_codes[u][:], table_words[:].bitcast(U32).indirect(offs_sb[:, 32 * u : 32 * (u + 1)]))
+
+        w1_cols = w1_raw[:].rearrange("p j (m t) -> p t m j", t=PACK)
+        w1_bf = [keep.tile([P, P, PACK], BF16, name="w1_bf%d" % t, align_bytes=64) for t in range(PACK)]
+        w1_codes = [keep.tile([P, P], U32, name="w1_codes%d" % t, align_bytes=64) for t in range(PACK)]
+        w1_scale = [keep.tile([P, P], U8, name="w1_scale%d" % t, align_bytes=64) for t in range(PACK)]
+        h = [keep.tile([P, S], F32, name="h%d" % t, align_bytes=64) for t in range(PACK)]
+
+        def quantise(codes, scale, values):
+            nc.vector.quantize_mx(out=codes.bitcast(FP8X4), scales=scale, in_=values.rearrange("p c j -> p (c j)"))
+
+        nc.vector.tensor_copy(w1_bf[0][:], w1_cols[:, 0])
+        for t in range(1, PACK):
+            nc.scalar.copy(w1_bf[t][:], w1_cols[:, t])
+        for t in range(PACK):
+            quantise(w1_codes[t][:], w1_scale[t][:], w1_bf[t][:])
+            for u in range(2):
+                acc = psum.tile([P, BANK], F32, name="acc", tag="acc%d" % ((2 * t + u) % 5))
+                nc.tensor.matmul_mx(
+                    out=acc[:],
+                    lhsT=w1_codes[t][:].bitcast(FP8X4),
+                    lhsT_scale=w1_scale[t][:],
+                    rhs=x_codes[u][:].bitcast(FP8X4),
+                    rhs_scale=x_scale[:, u * BANK : (u + 1) * BANK],
+                    start=True,
+                    stop=True,
+                )
+                if t == 0 and u == 0:
+                    nc.vector.tensor_scalar_max(h[t][:, u * BANK : (u + 1) * BANK], acc[:], 0.0)
+                else:
+                    nc.scalar.activation(h[t][:, u * BANK : (u + 1) * BANK], acc[:], RELU)
+
+        w23_bf = keep.tile([P, 2 * N, PACK], BF16, name="w23_bf", align_bytes=64)
+        w23_codes = keep.tile([P, 2 * N], U32, name="w23_codes", align_bytes=64)
+        w23_scale = keep.tile([P, 2 * N], U8, name="w23_scale", align_bytes=64)
+        nc.scalar.copy(w23_bf[:, :N, :], w2_raw[:].rearrange("p j c -> p c j"))
+        nc.scalar.copy(w23_bf[:, N:, :], w3_raw[:].rearrange("p j c -> p c j"))
+
+        own = keep.tile([P, PACK, V], BF16, name="own", align_bytes=64)
+        nbr = [keep.tile([P, PACK, V], BF16, name="nbr%d" % d, align_bytes=64) for d in range(3)]
+        pair = keep.tile([P, PACK, V], BF16, name="pair", align_bytes=64)
+        top = keep.tile([P, PACK, V], BF16, name="top", align_bytes=64)
+
+        def fetch(dst, idx, t, a, b):
+            nc.vector.tensor_copy(dst[:, t, a:b], h[t][:].indirect(idx[:, a // 16 : b // 16]))
+
+        def largest(t0, t1, a, b):
+            nc.vector.tensor_tensor(pair[:, t0:t1, a:b], nbr[0][:, t0:t1, a:b], nbr[1][:, t0:t1, a:b], MAX)
+            return lambda: nc.vector.tensor_tensor(top[:, t0:t1, a:b], pair[:, t0:t1, a:b], nbr[2][:, t0:t1, a:b], MAX)
+
+        for t in range(2):
+            for d in range(3):
+                fetch(nbr[d], pos_sb[d], t, 0, V)
+            fetch(own, cen_sb, t, 0, V)
+        finish = largest(0, 2, 0, V)
+        quantise(w23_codes[:], w23_scale[:], w23_bf[:])
+        finish()
+
+        for a, b in CHUNKS:
+            n = b - a
+            for d in range(3):
+                for t in range(2, PACK):
+                    fetch(nbr[d], pos_sb[d], t, a, b)
+            finish = largest(2, PACK, a, b)
+            fetch(own, cen_sb, 2, a, b)
+            finish()
+            fetch(own, cen_sb, 3, a, b)
+            acc = psum.tile([P, n], F32, name="res", tag="res%d" % a)
+            for i, src in enumerate((top, own)):
+                woven = keep.tile([P, n, PACK], BF16, name="woven%d_%d" % (i, a), align_bytes=64)
+                codes = keep.tile([P, n], U32, name="codes%d_%d" % (i, a), align_bytes=64)
+                scale = keep.tile([P, n], U8, name="scale%d_%d" % (i, a), align_bytes=64)
+                nc.scalar.copy(woven[:], src[:, :, a:b].rearrange("p t v -> p v t"))
+                quantise(codes[:], scale[:], woven[:])
+                cols = slice(N, 2 * N) if i == 0 else slice(0, N)
+                nc.tensor.matmul_mx(
+                    out=acc[:],
+                    lhsT=w23_codes[:, cols].bitcast(FP8X4),
+                    lhsT_scale=w23_scale[:, cols],
+                    rhs=codes[:].bitcast(FP8X4),
+                    rhs_scale=scale[:],
+                    start=(i == 0),
+                    stop=(i == 1),
+                )
+            res = keep.tile([P, n], F32, name="res_sb%d" % a, align_bytes=64)
+            nc.scalar.activation(res[:], acc[:], RELU)
+            nc.sync.dma_start(out[:, a:b], res[:])

@@ -19,6 +19,7 @@ P = 128
 PACK = 4
 BANK = 512
 HEAD_COLS = 1024
+H_BANKS = 5
 CHUNKS = ((0, 256), (256, 384), (384, 512))
 
 
@@ -33,113 +34,159 @@ def tile_picked_sagecat_maxrelu_p_kernel(tc, x_words, x_scales, w1, w2, w3, offs
         pos_sb = [keep.tile([P, V // 16], U16, name="pos_sb%d" % d) for d in range(3)]
         table_words = keep.tile([P, T], I32, name="table_words", align_bytes=64)
         table_scales = keep.tile([P, T], U8, name="table_scales", align_bytes=64)
-        w1_raw = keep.tile([P, PACK, H], F32, name="w1_raw", align_bytes=64)
-        w2_raw = keep.tile([P, PACK, N], F32, name="w2_raw", align_bytes=64)
-        w3_raw = keep.tile([P, PACK, N], F32, name="w3_raw", align_bytes=64)
+        x_scale = keep.tile([P, S], U8, name="x_scale", align_bytes=64)
+        w1_raw = [keep.tile([P, 2, H], F32, name="w1_raw%d" % e, tag="raw%d" % e, align_bytes=64) for e in range(2)]
 
         nc.vector.memset(table_scales[:].bitcast(I32), 0)
+        nc.vector.memset(x_scale[:].bitcast(I32), 0)
+        warm = keep.tile([P, 2], F32, name="warm")
+        nc.gpsimd.memset(warm[:, 0:1], 0.0)
+        nc.scalar.activation(warm[:, 1:2], warm[:, 0:1], RELU)
         words_hbm = x_words[0].rearrange("p c r -> p (c r)").bitcast(I32)
-        scales_hbm = x_scales[0].bitcast(I32)
+        w1_rows = w1.rearrange("(p j) c -> p j c", j=PACK)
         nc.sync.dma_start(offs_sb[:], offs)
         nc.sync.dma_start(table_words[:, :HEAD_COLS], words_hbm[:, :HEAD_COLS])
-        for q in range(4):
-            nc.sync.dma_start(table_scales[32 * q : 32 * q + 4, :].bitcast(I32), scales_hbm[4 * q : 4 * q + 4, :])
-        nc.sync.dma_start(table_words[:, HEAD_COLS:], words_hbm[:, HEAD_COLS:])
-        nc.sync.dma_start(w1_raw[:], w1.rearrange("(p j) c -> p j c", j=PACK))
-        for d, pos in enumerate((pos1, pos2, pos3)):
-            nc.sync.dma_start(pos_sb[d][:], pos)
         nc.sync.dma_start(cen_sb[:], cen)
-        nc.sync.dma_start(w2_raw[:], w2.rearrange("(p j) c -> p j c", j=PACK))
-        nc.sync.dma_start(w3_raw[:], w3.rearrange("(p j) c -> p j c", j=PACK))
+        nc.sync.dma_start(pos_sb[0][:], pos1)
+        nc.sync.dma_start(pos_sb[1][:], pos2)
+        nc.sync.dma_start(table_scales[0:P:8, :].bitcast(I32), x_scales[0].bitcast(I32))
+        nc.sync.dma_start(table_words[:, HEAD_COLS:], words_hbm[:, HEAD_COLS:])
+        for e in range(2):
+            nc.sync.dma_start(w1_raw[e][:], w1_rows[:, 2 * e : 2 * e + 2, :])
+        nc.sync.dma_start(pos_sb[2][:], pos3)
 
-        x_scale = keep.tile([P, S], U8, name="x_scale", align_bytes=64)
-        nc.vector.tensor_copy(x_scale[:], table_scales[:].indirect(offs_sb[:]))
+        picked_scale = keep.tile([P, S], U8, name="picked_scale", align_bytes=64)
+        nc.vector.tensor_copy(picked_scale[:], table_scales[:].indirect(offs_sb[:]))
+        for q in range(4):
+            nc.scalar.dma_start(x_scale[32 * q : 32 * q + 4, :].bitcast(I32), picked_scale[32 * q : 32 * q + 32 : 8, :].bitcast(I32))
         x_codes = [keep.tile([P, BANK], U32, name="x_codes%d" % u, align_bytes=64) for u in range(2)]
         for u in range(2):
             nc.vector.tensor_copy(x_codes[u][:], table_words[:].bitcast(U32).indirect(offs_sb[:, 32 * u : 32 * (u + 1)]))
 
-        w1_cols = w1_raw[:].rearrange("p j (m t) -> p t m j", t=PACK)
-        w1_bf = [keep.tile([P, P, PACK], BF16, name="w1_bf%d" % t, align_bytes=64) for t in range(PACK)]
-        w1_codes = [keep.tile([P, P], U32, name="w1_codes%d" % t, align_bytes=64) for t in range(PACK)]
-        w1_scale = [keep.tile([P, P], U8, name="w1_scale%d" % t, align_bytes=64) for t in range(PACK)]
+        w1_bf = [keep.tile([P, P, PACK], BF16, name="w1_bf%d" % t, tag="w1_bf%d" % (t % 2), align_bytes=64) for t in range(PACK)]
+        w1_codes = [keep.tile([P, P], U32, name="w1_codes%d" % t, tag="w1_codes%d" % (t % 2), align_bytes=64) for t in range(PACK)]
+        w1_scale = [keep.tile([P, P], U8, name="w1_scale%d" % t, tag="w1_scale%d" % (t % 2), align_bytes=64) for t in range(PACK)]
         h = [keep.tile([P, S], F32, name="h%d" % t, align_bytes=64) for t in range(PACK)]
 
         def quantise(codes, scale, values):
             nc.vector.quantize_mx(out=codes.bitcast(FP8X4), scales=scale, in_=values.rearrange("p c j -> p (c j)"))
 
-        nc.vector.tensor_copy(w1_bf[0][:], w1_cols[:, 0])
-        for t in range(1, PACK):
-            nc.scalar.copy(w1_bf[t][:], w1_cols[:, t])
+        def weave(dst, src):
+            nc.scalar.copy(dst.rearrange("p (c i) j -> p c j i", i=4), src.rearrange("p j (c i) -> p c j i", i=4))
+
+        def round_w1(t, e):
+            dst = w1_bf[t][:, :, 2 * e : 2 * e + 2]
+            src = w1_raw[e][:].rearrange("p j (m t) -> p t m j", t=PACK)[:, t]
+            if t == 0 and e == 1:
+                nc.vector.tensor_copy(dst, src)
+            else:
+                nc.scalar.copy(dst, src)
+
+        banks = []
+
+        def first_product(t, a, b, on_vector):
+            acc = psum.tile([P, b - a], F32, name="acc", tag="acc%d" % (len(banks) % H_BANKS))
+            banks.append(acc)
+            u, c = divmod(a, BANK)
+            nc.tensor.matmul_mx(
+                out=acc[:],
+                lhsT=w1_codes[t][:].bitcast(FP8X4),
+                lhsT_scale=w1_scale[t][:],
+                rhs=x_codes[u][:, c : c + b - a].bitcast(FP8X4),
+                rhs_scale=x_scale[:, a:b],
+                start=True,
+                stop=True,
+            )
+            if on_vector:
+                nc.vector.tensor_scalar_max(h[t][:, a:b], acc[:], 0.0)
+            else:
+                nc.scalar.activation(h[t][:, a:b], acc[:], RELU)
+
         for t in range(PACK):
+            round_w1(t, 0)
+            round_w1(t, 1)
             quantise(w1_codes[t][:], w1_scale[t][:], w1_bf[t][:])
-            for u in range(2):
-                acc = psum.tile([P, BANK], F32, name="acc", tag="acc%d" % ((2 * t + u) % 5))
-                nc.tensor.matmul_mx(
-                    out=acc[:],
-                    lhsT=w1_codes[t][:].bitcast(FP8X4),
-                    lhsT_scale=w1_scale[t][:],
-                    rhs=x_codes[u][:].bitcast(FP8X4),
-                    rhs_scale=x_scale[:, u * BANK : (u + 1) * BANK],
-                    start=True,
-                    stop=True,
-                )
-                if t == 0 and u == 0:
-                    nc.vector.tensor_scalar_max(h[t][:, u * BANK : (u + 1) * BANK], acc[:], 0.0)
-                else:
-                    nc.scalar.activation(h[t][:, u * BANK : (u + 1) * BANK], acc[:], RELU)
+            width = BANK // 2 if t == 0 else BANK
+            for i, a in enumerate(range(0, S, width)):
+                first_product(t, a, a + width, t == 0)
 
         w23_bf = keep.tile([P, 2 * N, PACK], BF16, name="w23_bf", align_bytes=64)
         w23_codes = keep.tile([P, 2 * N], U32, name="w23_codes", align_bytes=64)
         w23_scale = keep.tile([P, 2 * N], U8, name="w23_scale", align_bytes=64)
-        nc.scalar.copy(w23_bf[:, :N, :], w2_raw[:].rearrange("p j c -> p c j"))
-        nc.scalar.copy(w23_bf[:, N:, :], w3_raw[:].rearrange("p j c -> p c j"))
+        for e, w in enumerate((w2, w3)):
+            raw = keep.tile([P, PACK, N], F32, name="w23_raw%d" % e, tag="raw%d" % e, align_bytes=64)
+            nc.sync.dma_start(raw[:], w.rearrange("(p j) c -> p j c", j=PACK))
+            weave(w23_bf[:, e * N : (e + 1) * N, :], raw[:])
 
         own = keep.tile([P, PACK, V], BF16, name="own", align_bytes=64)
         nbr = [keep.tile([P, PACK, V], BF16, name="nbr%d" % d, align_bytes=64) for d in range(3)]
         pair = keep.tile([P, PACK, V], BF16, name="pair", align_bytes=64)
-        top = keep.tile([P, PACK, V], BF16, name="top", align_bytes=64)
+        top = keep.tile([P, PACK, V], BF16, name="top", tag="top", align_bytes=64)
 
         def fetch(dst, idx, t, a, b):
             nc.vector.tensor_copy(dst[:, t, a:b], h[t][:].indirect(idx[:, a // 16 : b // 16]))
 
-        def largest(t0, t1, a, b):
-            nc.vector.tensor_tensor(pair[:, t0:t1, a:b], nbr[0][:, t0:t1, a:b], nbr[1][:, t0:t1, a:b], MAX)
-            return lambda: nc.vector.tensor_tensor(top[:, t0:t1, a:b], pair[:, t0:t1, a:b], nbr[2][:, t0:t1, a:b], MAX)
+        def larger(dst, x, y, t0, t1, a, b):
+            nc.vector.tensor_tensor(dst[:, t0:t1, a:b], x[:, t0:t1, a:b], y[:, t0:t1, a:b], MAX)
 
         for t in range(2):
             for d in range(3):
                 fetch(nbr[d], pos_sb[d], t, 0, V)
             fetch(own, cen_sb, t, 0, V)
-        finish = largest(0, 2, 0, V)
-        quantise(w23_codes[:], w23_scale[:], w23_bf[:])
-        finish()
+        larger(pair, nbr[0], nbr[1], 0, 2, 0, V)
+        fetch(own, cen_sb, 2, 0, V)
+        larger(top, pair, nbr[2], 0, 2, 0, V)
+        fetch(own, cen_sb, 3, 0, V)
 
+        own_bf = keep.tile([P, V, PACK], BF16, name="own_bf", align_bytes=64)
+        own_codes = keep.tile([P, V], U32, name="own_codes", align_bytes=64)
+        own_scale = keep.tile([P, V], U8, name="own_scale", align_bytes=64)
+        weave(own_bf[:], own[:])
+
+        top_bf = []
         for a, b in CHUNKS:
-            n = b - a
-            for d in range(3):
+            for d in range(2):
                 for t in range(2, PACK):
                     fetch(nbr[d], pos_sb[d], t, a, b)
-            finish = largest(2, PACK, a, b)
-            fetch(own, cen_sb, 2, a, b)
-            finish()
-            fetch(own, cen_sb, 3, a, b)
-            acc = psum.tile([P, n], F32, name="res", tag="res%d" % a)
-            for i, src in enumerate((top, own)):
-                woven = keep.tile([P, n, PACK], BF16, name="woven%d_%d" % (i, a), align_bytes=64)
-                codes = keep.tile([P, n], U32, name="codes%d_%d" % (i, a), align_bytes=64)
-                scale = keep.tile([P, n], U8, name="scale%d_%d" % (i, a), align_bytes=64)
-                nc.scalar.copy(woven[:], src[:, :, a:b].rearrange("p t v -> p v t"))
-                quantise(codes[:], scale[:], woven[:])
-                cols = slice(N, 2 * N) if i == 0 else slice(0, N)
-                nc.tensor.matmul_mx(
-                    out=acc[:],
-                    lhsT=w23_codes[:, cols].bitcast(FP8X4),
-                    lhsT_scale=w23_scale[:, cols],
-                    rhs=codes[:].bitcast(FP8X4),
-                    rhs_scale=scale[:],
-                    start=(i == 0),
-                    stop=(i == 1),
-                )
-            res = keep.tile([P, n], F32, name="res_sb%d" % a, align_bytes=64)
-            nc.scalar.activation(res[:], acc[:], RELU)
-            nc.sync.dma_start(out[:, a:b], res[:])
+            fetch(nbr[2], pos_sb[2], 2, a, b)
+            larger(pair, nbr[0], nbr[1], 2, PACK, a, b)
+            fetch(nbr[2], pos_sb[2], 3, a, b)
+            larger(top, pair, nbr[2], 2, PACK, a, b)
+            woven = keep.tile([P, b - a, PACK], BF16, name="top_bf%d" % a, align_bytes=64)
+            weave(woven[:], top[:, :, a:b])
+            top_bf.append(woven)
+
+        quantise(w23_codes[:], w23_scale[:], w23_bf[:])
+        quantise(own_codes[:], own_scale[:], own_bf[:])
+        last = CHUNKS[-1][0]
+        early_acc = psum.tile([P, last], F32, name="early_acc")
+        last_acc = psum.tile([P, V - last], F32, name="last_acc")
+        for (a, b), woven in zip(CHUNKS, top_bf):
+            codes = keep.tile([P, b - a], U32, name="top_codes%d" % a, align_bytes=64)
+            scale = keep.tile([P, b - a], U8, name="top_scale%d" % a, align_bytes=64)
+            quantise(codes[:], scale[:], woven[:])
+            acc = last_acc[:] if a == last else early_acc[:, a:b]
+            nc.tensor.matmul_mx(
+                out=acc,
+                lhsT=w23_codes[:, :N].bitcast(FP8X4),
+                lhsT_scale=w23_scale[:, :N],
+                rhs=own_codes[:, a:b].bitcast(FP8X4),
+                rhs_scale=own_scale[:, a:b],
+                start=True,
+                stop=False,
+            )
+            nc.tensor.matmul_mx(
+                out=acc,
+                lhsT=w23_codes[:, N:].bitcast(FP8X4),
+                lhsT_scale=w23_scale[:, N:],
+                rhs=codes[:].bitcast(FP8X4),
+                rhs_scale=scale[:],
+                start=False,
+                stop=True,
+            )
+        early = keep.tile([P, last], F32, name="early", tag="top", align_bytes=64)
+        nc.scalar.activation(early[:], early_acc[:], RELU)
+        nc.scalar.dma_start(out[:, :last], early[:])
+        late = keep.tile([P, V - last], F32, name="late", align_bytes=64)
+        nc.vector.tensor_scalar_max(late[:], last_acc[:], 0.0)
+        nc.sync.dma_start(out[:, last:], late[:])

@@ -21,12 +21,14 @@ BANK = 512
 HEAD_COLS = 1024
 H_BANKS = 5
 CHUNKS = ((0, 256), (256, 384), (384, 512))
+LAST = 384
 
 
 def tile_picked_sagecat_maxrelu_p_kernel(tc, x_words, x_scales, w1, w2, w3, offs, cen, pos1, pos2, pos3, out):
     nc = tc.nc
     with ExitStack() as ctx:
         keep = ctx.enter_context(tc.tile_pool(name="keep", bufs=1))
+        ring = ctx.enter_context(tc.tile_pool(name="ring", bufs=2))
         psum = ctx.enter_context(tc.psum_pool(name="psum", bufs=1))
 
         offs_sb = keep.tile([P, S // 16], U16, name="offs_sb")
@@ -39,13 +41,10 @@ def tile_picked_sagecat_maxrelu_p_kernel(tc, x_words, x_scales, w1, w2, w3, offs
 
         nc.vector.memset(table_scales[:].bitcast(I32), 0)
         nc.vector.memset(x_scale[:].bitcast(I32), 0)
-        warm = keep.tile([P, 2], F32, name="warm")
-        nc.gpsimd.memset(warm[:, 0:1], 0.0)
-        nc.scalar.activation(warm[:, 1:2], warm[:, 0:1], RELU)
         words_hbm = x_words[0].rearrange("p c r -> p (c r)").bitcast(I32)
         w1_rows = w1.rearrange("(p j) c -> p j c", j=PACK)
-        nc.sync.dma_start(offs_sb[:], offs)
         nc.sync.dma_start(table_words[:, :HEAD_COLS], words_hbm[:, :HEAD_COLS])
+        nc.sync.dma_start(offs_sb[:], offs)
         nc.sync.dma_start(cen_sb[:], cen)
         nc.sync.dma_start(pos_sb[0][:], pos1)
         nc.sync.dma_start(pos_sb[1][:], pos2)
@@ -129,22 +128,33 @@ def tile_picked_sagecat_maxrelu_p_kernel(tc, x_words, x_scales, w1, w2, w3, offs
         def larger(dst, x, y, t0, t1, a, b):
             nc.vector.tensor_tensor(dst[:, t0:t1, a:b], x[:, t0:t1, a:b], y[:, t0:t1, a:b], MAX)
 
-        for t in range(2):
-            for d in range(3):
-                fetch(nbr[d], pos_sb[d], t, 0, V)
-            fetch(own, cen_sb, t, 0, V)
-        larger(pair, nbr[0], nbr[1], 0, 2, 0, V)
-        fetch(own, cen_sb, 2, 0, V)
-        larger(top, pair, nbr[2], 0, 2, 0, V)
-        fetch(own, cen_sb, 3, 0, V)
+        def larger_aside(dst, x, y, t, final):
+            if final:
+                lead = keep.tile([P, V], F32, name="last_lead", tag="last_lead", align_bytes=64)
+            else:
+                lead = ring.tile([P, V], F32, name="lead")
+            gain = ring.tile([P, V], F32, name="gain")
+            nc.gpsimd.tensor_tensor(lead[:], y[:, t, :], x[:, t, :], mybir.AluOpType.subtract)
+            nc.scalar.activation(gain[:], lead[:], RELU)
+            nc.gpsimd.tensor_tensor(dst[:, t, :], gain[:], x[:, t, :], mybir.AluOpType.add)
 
-        own_bf = keep.tile([P, V, PACK], BF16, name="own_bf", align_bytes=64)
+        for t in range(2):
+            for d in range(2):
+                fetch(nbr[d], pos_sb[d], t, 0, V)
+            larger_aside(pair, nbr[0], nbr[1], t, False)
+        for t in range(2):
+            fetch(nbr[2], pos_sb[2], t, 0, V)
+            larger_aside(top, pair, nbr[2], t, t == 1)
+        for t in range(PACK):
+            fetch(own, cen_sb, t, 0, V)
+
+        own_bf = keep.tile([P, V, PACK], BF16, name="own_bf", tag="last_lead", align_bytes=64)
         own_codes = keep.tile([P, V], U32, name="own_codes", align_bytes=64)
         own_scale = keep.tile([P, V], U8, name="own_scale", align_bytes=64)
         weave(own_bf[:], own[:])
 
-        top_bf = []
-        for a, b in CHUNKS:
+        top_bf = {}
+        for a, b in ((0, LAST), (LAST, V)):
             for d in range(2):
                 for t in range(2, PACK):
                     fetch(nbr[d], pos_sb[d], t, a, b)
@@ -152,19 +162,20 @@ def tile_picked_sagecat_maxrelu_p_kernel(tc, x_words, x_scales, w1, w2, w3, offs
             larger(pair, nbr[0], nbr[1], 2, PACK, a, b)
             fetch(nbr[2], pos_sb[2], 3, a, b)
             larger(top, pair, nbr[2], 2, PACK, a, b)
-            woven = keep.tile([P, b - a, PACK], BF16, name="top_bf%d" % a, align_bytes=64)
-            weave(woven[:], top[:, :, a:b])
-            top_bf.append(woven)
+            for c, e in CHUNKS:
+                if a <= c < b:
+                    top_bf[c] = keep.tile([P, e - c, PACK], BF16, name="top_bf%d" % c, align_bytes=64)
+                    weave(top_bf[c][:], top[:, :, c:e])
 
         quantise(w23_codes[:], w23_scale[:], w23_bf[:])
         quantise(own_codes[:], own_scale[:], own_bf[:])
         last = CHUNKS[-1][0]
         early_acc = psum.tile([P, last], F32, name="early_acc")
         last_acc = psum.tile([P, V - last], F32, name="last_acc")
-        for (a, b), woven in zip(CHUNKS, top_bf):
+        for a, b in CHUNKS:
             codes = keep.tile([P, b - a], U32, name="top_codes%d" % a, align_bytes=64)
             scale = keep.tile([P, b - a], U8, name="top_scale%d" % a, align_bytes=64)
-            quantise(codes[:], scale[:], woven[:])
+            quantise(codes[:], scale[:], top_bf[a][:])
             acc = last_acc[:] if a == last else early_acc[:, a:b]
             nc.tensor.matmul_mx(
                 out=acc,

@@ -13,15 +13,21 @@ U16 = mybir.dt.uint16
 U8 = mybir.dt.uint8
 FP8X4 = mybir.dt.float8_e4m3fn_x4
 MAX = mybir.AluOpType.max
+ADD = mybir.AluOpType.add
+SUBTRACT = mybir.AluOpType.subtract
 RELU = mybir.ActivationFunctionType.Relu
 
 P = 128
 PACK = 4
+BLOCK_ROWS = 8
+QUADRANT = 32
+PER_COLUMN = 16
 BANK = 512
-HEAD_COLS = 1024
 H_BANKS = 5
-CHUNKS = ((0, 256), (256, 384), (384, 512))
+HEAD_COLS = 1024
+SIDE_PLANES = 2
 LAST = 384
+CHUNKS = ((0, 256), (256, LAST), (LAST, V))
 
 
 def tile_picked_sagecat_maxrelu_p_kernel(tc, x_words, x_scales, w1, w2, w3, offs, cen, pos1, pos2, pos3, out):
@@ -31,9 +37,9 @@ def tile_picked_sagecat_maxrelu_p_kernel(tc, x_words, x_scales, w1, w2, w3, offs
         ring = ctx.enter_context(tc.tile_pool(name="ring", bufs=2))
         psum = ctx.enter_context(tc.psum_pool(name="psum", bufs=1))
 
-        offs_sb = keep.tile([P, S // 16], U16, name="offs_sb")
-        cen_sb = keep.tile([P, V // 16], U16, name="cen_sb")
-        pos_sb = [keep.tile([P, V // 16], U16, name="pos_sb%d" % d) for d in range(3)]
+        offs_sb = keep.tile([P, S // PER_COLUMN], U16, name="offs_sb")
+        cen_sb = keep.tile([P, V // PER_COLUMN], U16, name="cen_sb")
+        pos_sb = [keep.tile([P, V // PER_COLUMN], U16, name="pos_sb%d" % d) for d in range(3)]
         table_words = keep.tile([P, T], I32, name="table_words", align_bytes=64)
         table_scales = keep.tile([P, T], U8, name="table_scales", align_bytes=64)
         x_scale = keep.tile([P, S], U8, name="x_scale", align_bytes=64)
@@ -48,7 +54,7 @@ def tile_picked_sagecat_maxrelu_p_kernel(tc, x_words, x_scales, w1, w2, w3, offs
         nc.sync.dma_start(cen_sb[:], cen)
         nc.sync.dma_start(pos_sb[0][:], pos1)
         nc.sync.dma_start(pos_sb[1][:], pos2)
-        nc.sync.dma_start(table_scales[0:P:8, :].bitcast(I32), x_scales[0].bitcast(I32))
+        nc.sync.dma_start(table_scales[0:P:BLOCK_ROWS, :].bitcast(I32), x_scales[0].bitcast(I32))
         nc.sync.dma_start(table_words[:, HEAD_COLS:], words_hbm[:, HEAD_COLS:])
         for e in range(2):
             nc.sync.dma_start(w1_raw[e][:], w1_rows[:, 2 * e : 2 * e + 2, :])
@@ -56,19 +62,23 @@ def tile_picked_sagecat_maxrelu_p_kernel(tc, x_words, x_scales, w1, w2, w3, offs
 
         picked_scale = keep.tile([P, S], U8, name="picked_scale", align_bytes=64)
         nc.vector.tensor_copy(picked_scale[:], table_scales[:].indirect(offs_sb[:]))
-        for q in range(4):
-            nc.scalar.dma_start(x_scale[32 * q : 32 * q + 4, :].bitcast(I32), picked_scale[32 * q : 32 * q + 32 : 8, :].bitcast(I32))
-        x_codes = [keep.tile([P, BANK], U32, name="x_codes%d" % u, align_bytes=64) for u in range(2)]
-        for u in range(2):
-            nc.vector.tensor_copy(x_codes[u][:], table_words[:].bitcast(U32).indirect(offs_sb[:, 32 * u : 32 * (u + 1)]))
+        for first in range(0, P, QUADRANT):
+            nc.scalar.dma_start(
+                x_scale[first : first + QUADRANT // BLOCK_ROWS, :].bitcast(I32),
+                picked_scale[first : first + QUADRANT : BLOCK_ROWS, :].bitcast(I32),
+            )
+        x_codes = [keep.tile([P, BANK], U32, name="x_codes%d" % u, align_bytes=64) for u in range(S // BANK)]
+        for u in range(S // BANK):
+            entries = offs_sb[:, u * BANK // PER_COLUMN : (u + 1) * BANK // PER_COLUMN]
+            nc.vector.tensor_copy(x_codes[u][:], table_words[:].bitcast(U32).indirect(entries))
 
         w1_bf = [keep.tile([P, P, PACK], BF16, name="w1_bf%d" % t, tag="w1_bf%d" % (t % 2), align_bytes=64) for t in range(PACK)]
         w1_codes = [keep.tile([P, P], U32, name="w1_codes%d" % t, tag="w1_codes%d" % (t % 2), align_bytes=64) for t in range(PACK)]
         w1_scale = [keep.tile([P, P], U8, name="w1_scale%d" % t, tag="w1_scale%d" % (t % 2), align_bytes=64) for t in range(PACK)]
         h = [keep.tile([P, S], F32, name="h%d" % t, align_bytes=64) for t in range(PACK)]
 
-        def quantise(codes, scale, values):
-            nc.vector.quantize_mx(out=codes.bitcast(FP8X4), scales=scale, in_=values.rearrange("p c j -> p (c j)"))
+        def quantise(codes, scale, woven):
+            nc.vector.quantize_mx(out=codes.bitcast(FP8X4), scales=scale, in_=woven.rearrange("p c j -> p (c j)"))
 
         def weave(dst, src):
             nc.scalar.copy(dst.rearrange("p (c i) j -> p c j i", i=4), src.rearrange("p j (c i) -> p c j i", i=4))
@@ -83,7 +93,7 @@ def tile_picked_sagecat_maxrelu_p_kernel(tc, x_words, x_scales, w1, w2, w3, offs
 
         banks = []
 
-        def first_product(t, a, b, on_vector):
+        def first_product(t, a, b):
             acc = psum.tile([P, b - a], F32, name="acc", tag="acc%d" % (len(banks) % H_BANKS))
             banks.append(acc)
             u, c = divmod(a, BANK)
@@ -96,7 +106,7 @@ def tile_picked_sagecat_maxrelu_p_kernel(tc, x_words, x_scales, w1, w2, w3, offs
                 start=True,
                 stop=True,
             )
-            if on_vector:
+            if t == 0:
                 nc.vector.tensor_scalar_max(h[t][:, a:b], acc[:], 0.0)
             else:
                 nc.scalar.activation(h[t][:, a:b], acc[:], RELU)
@@ -106,8 +116,8 @@ def tile_picked_sagecat_maxrelu_p_kernel(tc, x_words, x_scales, w1, w2, w3, offs
             round_w1(t, 1)
             quantise(w1_codes[t][:], w1_scale[t][:], w1_bf[t][:])
             width = BANK // 2 if t == 0 else BANK
-            for i, a in enumerate(range(0, S, width)):
-                first_product(t, a, a + width, t == 0)
+            for a in range(0, S, width):
+                first_product(t, a, a + width)
 
         w23_bf = keep.tile([P, 2 * N, PACK], BF16, name="w23_bf", align_bytes=64)
         w23_codes = keep.tile([P, 2 * N], U32, name="w23_codes", align_bytes=64)
@@ -123,10 +133,10 @@ def tile_picked_sagecat_maxrelu_p_kernel(tc, x_words, x_scales, w1, w2, w3, offs
         top = keep.tile([P, PACK, V], BF16, name="top", tag="top", align_bytes=64)
 
         def fetch(dst, idx, t, a, b):
-            nc.vector.tensor_copy(dst[:, t, a:b], h[t][:].indirect(idx[:, a // 16 : b // 16]))
+            nc.vector.tensor_copy(dst[:, t, a:b], h[t][:].indirect(idx[:, a // PER_COLUMN : b // PER_COLUMN]))
 
-        def larger(dst, x, y, t0, t1, a, b):
-            nc.vector.tensor_tensor(dst[:, t0:t1, a:b], x[:, t0:t1, a:b], y[:, t0:t1, a:b], MAX)
+        def larger(dst, x, y, a, b):
+            nc.vector.tensor_tensor(dst[:, SIDE_PLANES:, a:b], x[:, SIDE_PLANES:, a:b], y[:, SIDE_PLANES:, a:b], MAX)
 
         def larger_aside(dst, x, y, t, final):
             if final:
@@ -134,17 +144,17 @@ def tile_picked_sagecat_maxrelu_p_kernel(tc, x_words, x_scales, w1, w2, w3, offs
             else:
                 lead = ring.tile([P, V], F32, name="lead")
             gain = ring.tile([P, V], F32, name="gain")
-            nc.gpsimd.tensor_tensor(lead[:], y[:, t, :], x[:, t, :], mybir.AluOpType.subtract)
+            nc.gpsimd.tensor_tensor(lead[:], y[:, t, :], x[:, t, :], SUBTRACT)
             nc.scalar.activation(gain[:], lead[:], RELU)
-            nc.gpsimd.tensor_tensor(dst[:, t, :], gain[:], x[:, t, :], mybir.AluOpType.add)
+            nc.gpsimd.tensor_tensor(dst[:, t, :], gain[:], x[:, t, :], ADD)
 
-        for t in range(2):
+        for t in range(SIDE_PLANES):
             for d in range(2):
                 fetch(nbr[d], pos_sb[d], t, 0, V)
             larger_aside(pair, nbr[0], nbr[1], t, False)
-        for t in range(2):
+        for t in range(SIDE_PLANES):
             fetch(nbr[2], pos_sb[2], t, 0, V)
-            larger_aside(top, pair, nbr[2], t, t == 1)
+            larger_aside(top, pair, nbr[2], t, t == SIDE_PLANES - 1)
         for t in range(PACK):
             fetch(own, cen_sb, t, 0, V)
 
@@ -156,29 +166,25 @@ def tile_picked_sagecat_maxrelu_p_kernel(tc, x_words, x_scales, w1, w2, w3, offs
         top_bf = {}
         for a, b in ((0, LAST), (LAST, V)):
             for d in range(2):
-                for t in range(2, PACK):
+                for t in range(SIDE_PLANES, PACK):
                     fetch(nbr[d], pos_sb[d], t, a, b)
-            fetch(nbr[2], pos_sb[2], 2, a, b)
-            larger(pair, nbr[0], nbr[1], 2, PACK, a, b)
-            fetch(nbr[2], pos_sb[2], 3, a, b)
-            larger(top, pair, nbr[2], 2, PACK, a, b)
-            for c, e in CHUNKS:
-                if a <= c < b:
-                    top_bf[c] = keep.tile([P, e - c, PACK], BF16, name="top_bf%d" % c, align_bytes=64)
-                    weave(top_bf[c][:], top[:, :, c:e])
+            fetch(nbr[2], pos_sb[2], PACK - 2, a, b)
+            larger(pair, nbr[0], nbr[1], a, b)
+            fetch(nbr[2], pos_sb[2], PACK - 1, a, b)
+            larger(top, pair, nbr[2], a, b)
+            for lo, hi in CHUNKS:
+                if a <= lo < b:
+                    top_bf[lo] = keep.tile([P, hi - lo, PACK], BF16, name="top_bf%d" % lo, align_bytes=64)
+                    weave(top_bf[lo][:], top[:, :, lo:hi])
 
         quantise(w23_codes[:], w23_scale[:], w23_bf[:])
-        quantise(own_codes[:], own_scale[:], own_bf[:])
-        last = CHUNKS[-1][0]
-        early_acc = psum.tile([P, last], F32, name="early_acc")
-        last_acc = psum.tile([P, V - last], F32, name="last_acc")
+        for a in range(0, V, V // 2):
+            quantise(own_codes[:, a : a + V // 2], own_scale[:, a : a + V // 2], own_bf[:, a : a + V // 2, :])
+        sums = {}
         for a, b in CHUNKS:
-            codes = keep.tile([P, b - a], U32, name="top_codes%d" % a, align_bytes=64)
-            scale = keep.tile([P, b - a], U8, name="top_scale%d" % a, align_bytes=64)
-            quantise(codes[:], scale[:], top_bf[a][:])
-            acc = last_acc[:] if a == last else early_acc[:, a:b]
+            sums[a] = psum.tile([P, b - a], F32, name="sum%d" % a)
             nc.tensor.matmul_mx(
-                out=acc,
+                out=sums[a][:],
                 lhsT=w23_codes[:, :N].bitcast(FP8X4),
                 lhsT_scale=w23_scale[:, :N],
                 rhs=own_codes[:, a:b].bitcast(FP8X4),
@@ -186,8 +192,14 @@ def tile_picked_sagecat_maxrelu_p_kernel(tc, x_words, x_scales, w1, w2, w3, offs
                 start=True,
                 stop=False,
             )
+        early = keep.tile([P, LAST], F32, name="early", tag="top", align_bytes=64)
+        late = keep.tile([P, V - LAST], F32, name="late", align_bytes=64)
+        for a, b in CHUNKS:
+            codes = keep.tile([P, b - a], U32, name="top_codes%d" % a, align_bytes=64)
+            scale = keep.tile([P, b - a], U8, name="top_scale%d" % a, align_bytes=64)
+            quantise(codes[:], scale[:], top_bf[a][:])
             nc.tensor.matmul_mx(
-                out=acc,
+                out=sums[a][:],
                 lhsT=w23_codes[:, N:].bitcast(FP8X4),
                 lhsT_scale=w23_scale[:, N:],
                 rhs=codes[:].bitcast(FP8X4),
@@ -195,9 +207,8 @@ def tile_picked_sagecat_maxrelu_p_kernel(tc, x_words, x_scales, w1, w2, w3, offs
                 start=False,
                 stop=True,
             )
-        early = keep.tile([P, last], F32, name="early", tag="top", align_bytes=64)
-        nc.scalar.activation(early[:], early_acc[:], RELU)
-        nc.scalar.dma_start(out[:, :last], early[:])
-        late = keep.tile([P, V - last], F32, name="late", align_bytes=64)
-        nc.vector.tensor_scalar_max(late[:], last_acc[:], 0.0)
-        nc.sync.dma_start(out[:, last:], late[:])
+        for a, b in CHUNKS[:-1]:
+            nc.scalar.activation(early[:, a:b], sums[a][:], RELU)
+        nc.scalar.dma_start(out[:, :LAST], early[:])
+        nc.vector.tensor_scalar_max(late[:], sums[LAST][:], 0.0)
+        nc.sync.dma_start(out[:, LAST:], late[:])

@@ -23,7 +23,7 @@ BLOCK_ROWS = 8
 QUADRANT = 32
 PER_COLUMN = 16
 BANK = 512
-H_BANKS = 5
+BANKS = 8
 HEAD_COLS = 1024
 SIDE_PLANES = 2
 LAST = 384
@@ -34,16 +34,15 @@ def tile_picked_sagecat_maxrelu_p_kernel(tc, x_words, x_scales, w1, w2, w3, offs
     nc = tc.nc
     with ExitStack() as ctx:
         keep = ctx.enter_context(tc.tile_pool(name="keep", bufs=1))
-        ring = ctx.enter_context(tc.tile_pool(name="ring", bufs=2))
         psum = ctx.enter_context(tc.psum_pool(name="psum", bufs=1))
 
         offs_sb = keep.tile([P, S // PER_COLUMN], U16, name="offs_sb")
         cen_sb = keep.tile([P, V // PER_COLUMN], U16, name="cen_sb")
         pos_sb = [keep.tile([P, V // PER_COLUMN], U16, name="pos_sb%d" % d) for d in range(3)]
-        table_words = keep.tile([P, T], I32, name="table_words", align_bytes=64)
+        table_words = keep.tile([P, T], I32, name="table_words", tag="table", align_bytes=64)
         table_scales = keep.tile([P, T], U8, name="table_scales", align_bytes=64)
         x_scale = keep.tile([P, S], U8, name="x_scale", align_bytes=64)
-        w1_raw = [keep.tile([P, 2, H], F32, name="w1_raw%d" % e, tag="raw%d" % e, align_bytes=64) for e in range(2)]
+        w1_raw = keep.tile([P, PACK, H], F32, name="w1_raw", tag="raw", align_bytes=64)
 
         nc.vector.memset(table_scales[:].bitcast(I32), 0)
         nc.vector.memset(x_scale[:].bitcast(I32), 0)
@@ -57,13 +56,13 @@ def tile_picked_sagecat_maxrelu_p_kernel(tc, x_words, x_scales, w1, w2, w3, offs
         nc.sync.dma_start(table_scales[0:P:BLOCK_ROWS, :].bitcast(I32), x_scales[0].bitcast(I32))
         nc.sync.dma_start(table_words[:, HEAD_COLS:], words_hbm[:, HEAD_COLS:])
         for e in range(2):
-            nc.sync.dma_start(w1_raw[e][:], w1_rows[:, 2 * e : 2 * e + 2, :])
+            nc.sync.dma_start(w1_raw[:, 2 * e : 2 * e + 2, :], w1_rows[:, 2 * e : 2 * e + 2, :])
         nc.sync.dma_start(pos_sb[2][:], pos3)
 
         picked_scale = keep.tile([P, S], U8, name="picked_scale", align_bytes=64)
         nc.vector.tensor_copy(picked_scale[:], table_scales[:].indirect(offs_sb[:]))
         for first in range(0, P, QUADRANT):
-            nc.scalar.dma_start(
+            nc.sync.dma_start(
                 x_scale[first : first + QUADRANT // BLOCK_ROWS, :].bitcast(I32),
                 picked_scale[first : first + QUADRANT : BLOCK_ROWS, :].bitcast(I32),
             )
@@ -72,9 +71,10 @@ def tile_picked_sagecat_maxrelu_p_kernel(tc, x_words, x_scales, w1, w2, w3, offs
             entries = offs_sb[:, u * BANK // PER_COLUMN : (u + 1) * BANK // PER_COLUMN]
             nc.vector.tensor_copy(x_codes[u][:], table_words[:].bitcast(U32).indirect(entries))
 
-        w1_bf = [keep.tile([P, P, PACK], BF16, name="w1_bf%d" % t, tag="w1_bf%d" % (t % 2), align_bytes=64) for t in range(PACK)]
-        w1_codes = [keep.tile([P, P], U32, name="w1_codes%d" % t, tag="w1_codes%d" % (t % 2), align_bytes=64) for t in range(PACK)]
-        w1_scale = [keep.tile([P, P], U8, name="w1_scale%d" % t, tag="w1_scale%d" % (t % 2), align_bytes=64) for t in range(PACK)]
+        groups = ((0, 1), (1, PACK))
+        w1_bf = [keep.tile([P, hi - lo, P, PACK], BF16, name="w1_bf%d" % lo, tag="w1_bf%d" % lo, align_bytes=64) for lo, hi in groups]
+        w1_codes = [keep.tile([P, hi - lo, P], U32, name="w1_codes%d" % lo, tag="w1_codes" if lo == 0 else "w1_bf0", align_bytes=64) for lo, hi in groups]
+        w1_scale = keep.tile([P, PACK, P], U8, name="w1_scale", align_bytes=64)
         h = [keep.tile([P, S], F32, name="h%d" % t, align_bytes=64) for t in range(PACK)]
 
         def quantise(codes, scale, woven):
@@ -83,106 +83,126 @@ def tile_picked_sagecat_maxrelu_p_kernel(tc, x_words, x_scales, w1, w2, w3, offs
         def weave(dst, src):
             nc.scalar.copy(dst.rearrange("p (c i) j -> p c j i", i=4), src.rearrange("p j (c i) -> p c j i", i=4))
 
-        def round_w1(t, e):
-            dst = w1_bf[t][:, :, 2 * e : 2 * e + 2]
-            src = w1_raw[e][:].rearrange("p j (m t) -> p t m j", t=PACK)[:, t]
-            if t == 0 and e == 1:
-                nc.vector.tensor_copy(dst, src)
-            else:
-                nc.scalar.copy(dst, src)
+        def round_w1(copy, g, j0, j1):
+            lo, hi = groups[g]
+            dst = w1_bf[g][:, :, :, j0:j1].rearrange("p t (b r) j -> p t b r j", r=BLOCK_ROWS)
+            src = w1_raw[:, j0:j1, :].rearrange("p j (b t r) -> p t b r j", t=PACK, r=BLOCK_ROWS)[:, lo:hi]
+            copy(dst, src)
+
+        def quantise_w1(g, lo, hi):
+            first = groups[g][0]
+            quantise(
+                w1_codes[g][:, lo - first : hi - first, :].rearrange("p t m -> p (t m)"),
+                w1_scale[:, lo:hi, :].rearrange("p t m -> p (t m)"),
+                w1_bf[g][:, lo - first : hi - first].rearrange("p t m j -> p (t m) j"),
+            )
 
         banks = []
 
-        def first_product(t, a, b):
-            acc = psum.tile([P, b - a], F32, name="acc", tag="acc%d" % (len(banks) % H_BANKS))
+        def next_bank(width, name):
+            acc = psum.tile([P, width], F32, name=name, tag="bank%d" % (len(banks) % BANKS))
             banks.append(acc)
+            return acc
+
+        def first_product(t, a, b):
+            acc = next_bank(b - a, "acc")
             u, c = divmod(a, BANK)
             nc.tensor.matmul_mx(
                 out=acc[:],
-                lhsT=w1_codes[t][:].bitcast(FP8X4),
-                lhsT_scale=w1_scale[t][:],
+                lhsT=w1_codes[min(t, 1)][:, max(t - 1, 0), :].bitcast(FP8X4),
+                lhsT_scale=w1_scale[:, t, :],
                 rhs=x_codes[u][:, c : c + b - a].bitcast(FP8X4),
                 rhs_scale=x_scale[:, a:b],
                 start=True,
                 stop=True,
             )
-            if t == 0:
+            if t == 0 and b == S:
                 nc.vector.tensor_scalar_max(h[t][:, a:b], acc[:], 0.0)
             else:
                 nc.scalar.activation(h[t][:, a:b], acc[:], RELU)
 
+        round_w1(nc.scalar.copy, 0, 0, 2)
+        round_w1(nc.vector.tensor_copy, 0, 2, PACK)
+        round_w1(nc.scalar.copy, 1, 0, 2)
+        round_w1(nc.scalar.copy, 1, 2, PACK)
+        quantise_w1(0, 0, 1)
+        quantise_w1(1, 1, 2)
+        quantise_w1(1, 2, PACK)
         for t in range(PACK):
-            round_w1(t, 0)
-            round_w1(t, 1)
-            quantise(w1_codes[t][:], w1_scale[t][:], w1_bf[t][:])
             width = BANK // 2 if t == 0 else BANK
             for a in range(0, S, width):
                 first_product(t, a, a + width)
 
         w23_bf = keep.tile([P, 2 * N, PACK], BF16, name="w23_bf", align_bytes=64)
-        w23_codes = keep.tile([P, 2 * N], U32, name="w23_codes", align_bytes=64)
         w23_scale = keep.tile([P, 2 * N], U8, name="w23_scale", align_bytes=64)
+        w23_raw = keep.tile([P, PACK, 2 * N], F32, name="w23_raw", tag="raw", align_bytes=64)
         for e, w in enumerate((w2, w3)):
-            raw = keep.tile([P, PACK, N], F32, name="w23_raw%d" % e, tag="raw%d" % e, align_bytes=64)
-            nc.sync.dma_start(raw[:], w.rearrange("(p j) c -> p j c", j=PACK))
-            weave(w23_bf[:, e * N : (e + 1) * N, :], raw[:])
+            for t in range(PACK):
+                nc.sync.dma_start(w23_raw[:, t, e * N : (e + 1) * N], w.rearrange("(b t r) c -> t b r c", t=PACK, r=BLOCK_ROWS)[t])
+        weave(w23_bf[:], w23_raw[:])
 
         own = keep.tile([P, PACK, V], BF16, name="own", align_bytes=64)
-        nbr = [keep.tile([P, PACK, V], BF16, name="nbr%d" % d, align_bytes=64) for d in range(3)]
-        pair = keep.tile([P, PACK, V], BF16, name="pair", align_bytes=64)
         top = keep.tile([P, PACK, V], BF16, name="top", tag="top", align_bytes=64)
 
         def fetch(dst, idx, t, a, b):
-            nc.vector.tensor_copy(dst[:, t, a:b], h[t][:].indirect(idx[:, a // PER_COLUMN : b // PER_COLUMN]))
+            nc.vector.tensor_copy(dst, h[t][:].indirect(idx[:, a // PER_COLUMN : b // PER_COLUMN]))
 
-        def larger(dst, x, y, a, b):
-            nc.vector.tensor_tensor(dst[:, SIDE_PLANES:, a:b], x[:, SIDE_PLANES:, a:b], y[:, SIDE_PLANES:, a:b], MAX)
+        def larger(dst, x, y):
+            nc.vector.tensor_tensor(dst, x, y, MAX)
 
-        def larger_aside(dst, x, y, t, final):
-            if final:
-                lead = keep.tile([P, V], F32, name="last_lead", tag="last_lead", align_bytes=64)
-            else:
-                lead = ring.tile([P, V], F32, name="lead")
-            gain = ring.tile([P, V], F32, name="gain")
-            nc.gpsimd.tensor_tensor(lead[:], y[:, t, :], x[:, t, :], SUBTRACT)
+        steps = []
+
+        def larger_aside(dst, x, y):
+            turn = len(steps) % 2
+            steps.append(dst)
+            lead = keep.tile([P, V], F32, name="lead", tag="lead%d" % turn, align_bytes=64)
+            gain = keep.tile([P, V], F32, name="gain", tag="gain%d" % turn, align_bytes=64)
+            nc.gpsimd.tensor_tensor(lead[:], y, x, SUBTRACT)
             nc.scalar.activation(gain[:], lead[:], RELU)
-            nc.gpsimd.tensor_tensor(dst[:, t, :], gain[:], x[:, t, :], ADD)
+            nc.gpsimd.tensor_tensor(dst, gain[:], x, ADD)
 
-        for t in range(SIDE_PLANES):
+        pair = [keep.tile([P, V], BF16, name="pair%d" % t, align_bytes=64) for t in range(PACK - 1)]
+        for t in range(PACK - 1):
+            nbr = [keep.tile([P, V], BF16, name="nbr", tag="nbr%d_%d" % (t, d), align_bytes=64) for d in range(2)]
             for d in range(2):
-                fetch(nbr[d], pos_sb[d], t, 0, V)
-            larger_aside(pair, nbr[0], nbr[1], t, False)
-        for t in range(SIDE_PLANES):
-            fetch(nbr[2], pos_sb[2], t, 0, V)
-            larger_aside(top, pair, nbr[2], t, t == SIDE_PLANES - 1)
-        for t in range(PACK):
-            fetch(own, cen_sb, t, 0, V)
+                fetch(nbr[d][:], pos_sb[d], t, 0, V)
+            larger_aside(pair[t][:], nbr[0][:], nbr[1][:])
+            if t < SIDE_PLANES:
+                third = keep.tile([P, V], BF16, name="third%d" % t, align_bytes=64)
+                fetch(third[:], pos_sb[2], t, 0, V)
+                larger_aside(top[:, t, :], pair[t][:], third[:])
+            fetch(own[:, t, :], cen_sb, t, 0, V)
+        fetch(own[:, PACK - 1, :], cen_sb, PACK - 1, 0, V)
+        last_turn = (len(steps) - 1) % 2
 
-        own_bf = keep.tile([P, V, PACK], BF16, name="own_bf", tag="last_lead", align_bytes=64)
+        own_bf = keep.tile([P, V, PACK], BF16, name="own_bf", tag="lead%d" % last_turn, align_bytes=64)
         own_codes = keep.tile([P, V], U32, name="own_codes", align_bytes=64)
         own_scale = keep.tile([P, V], U8, name="own_scale", align_bytes=64)
         weave(own_bf[:], own[:])
 
         top_bf = {}
         for a, b in ((0, LAST), (LAST, V)):
+            late = keep.tile([P, PACK, b - a], BF16, name="late", tag="late" if a == 0 else "nbr%d_0" % (PACK - 2), align_bytes=64)
+            pair3 = keep.tile([P, b - a], BF16, name="pair3", tag="gain%d" % last_turn if a == 0 else "pair3", align_bytes=64)
             for d in range(2):
-                for t in range(SIDE_PLANES, PACK):
-                    fetch(nbr[d], pos_sb[d], t, a, b)
-            fetch(nbr[2], pos_sb[2], PACK - 2, a, b)
-            larger(pair, nbr[0], nbr[1], a, b)
-            fetch(nbr[2], pos_sb[2], PACK - 1, a, b)
-            larger(top, pair, nbr[2], a, b)
+                fetch(late[:, d, :], pos_sb[d], PACK - 1, a, b)
+            for t in (PACK - 2, PACK - 1):
+                fetch(late[:, t, :], pos_sb[2], t, a, b)
+            larger(pair3[:], late[:, 0, :], late[:, 1, :])
+            larger(top[:, PACK - 2, a:b], pair[PACK - 2][:, a:b], late[:, PACK - 2, :])
+            larger(top[:, PACK - 1, a:b], pair3[:], late[:, PACK - 1, :])
             for lo, hi in CHUNKS:
                 if a <= lo < b:
                     top_bf[lo] = keep.tile([P, hi - lo, PACK], BF16, name="top_bf%d" % lo, align_bytes=64)
                     weave(top_bf[lo][:], top[:, :, lo:hi])
 
+        w23_codes = keep.tile([P, 2 * N], U32, name="w23_codes", tag="gain%d" % last_turn, align_bytes=64)
         quantise(w23_codes[:], w23_scale[:], w23_bf[:])
         for a in range(0, V, V // 2):
             quantise(own_codes[:, a : a + V // 2], own_scale[:, a : a + V // 2], own_bf[:, a : a + V // 2, :])
         sums = {}
         for a, b in CHUNKS:
-            sums[a] = psum.tile([P, b - a], F32, name="sum%d" % a)
+            sums[a] = next_bank(b - a, "sum%d" % a)
             nc.tensor.matmul_mx(
                 out=sums[a][:],
                 lhsT=w23_codes[:, :N].bitcast(FP8X4),
@@ -193,7 +213,7 @@ def tile_picked_sagecat_maxrelu_p_kernel(tc, x_words, x_scales, w1, w2, w3, offs
                 stop=False,
             )
         early = keep.tile([P, LAST], F32, name="early", tag="top", align_bytes=64)
-        late = keep.tile([P, V - LAST], F32, name="late", align_bytes=64)
+        ending = keep.tile([P, V - LAST], F32, name="ending", align_bytes=64)
         for a, b in CHUNKS:
             codes = keep.tile([P, b - a], U32, name="top_codes%d" % a, align_bytes=64)
             scale = keep.tile([P, b - a], U8, name="top_scale%d" % a, align_bytes=64)
@@ -210,5 +230,5 @@ def tile_picked_sagecat_maxrelu_p_kernel(tc, x_words, x_scales, w1, w2, w3, offs
         for a, b in CHUNKS[:-1]:
             nc.scalar.activation(early[:, a:b], sums[a][:], RELU)
         nc.scalar.dma_start(out[:, :LAST], early[:])
-        nc.vector.tensor_scalar_max(late[:], sums[LAST][:], 0.0)
-        nc.sync.dma_start(out[:, LAST:], late[:])
+        nc.vector.tensor_scalar_max(ending[:], sums[LAST][:], 0.0)
+        nc.sync.dma_start(out[:, LAST:], ending[:])

@@ -27,6 +27,8 @@ BANKS = 8
 HEAD_COLS = 1024
 SIDE_PLANES = 2
 LAST = 384
+GAIN_AT = 2 * 4 * V
+BASE_AT = 4 * 4 * V
 CHUNKS = ((0, 256), (256, LAST), (LAST, V))
 
 
@@ -34,6 +36,7 @@ def tile_picked_sagecat_maxrelu_p_kernel(tc, x_words, x_scales, w1, w2, w3, offs
     nc = tc.nc
     with ExitStack() as ctx:
         keep = ctx.enter_context(tc.tile_pool(name="keep", bufs=1))
+        placed = ctx.enter_context(tc.tile_pool(name="placed", bufs=1))
         psum = ctx.enter_context(tc.psum_pool(name="psum", bufs=1))
 
         offs_sb = keep.tile([P, S // PER_COLUMN], U16, name="offs_sb")
@@ -155,35 +158,40 @@ def tile_picked_sagecat_maxrelu_p_kernel(tc, x_words, x_scales, w1, w2, w3, offs
         def larger_aside(dst, x, y):
             turn = len(steps) % 2
             steps.append(dst)
-            lead = keep.tile([P, V], F32, name="lead", tag="lead%d" % turn, align_bytes=64)
-            gain = keep.tile([P, V], F32, name="gain", tag="gain%d" % turn, align_bytes=64)
+            lead = placed.tile([P, V], F32, name="lead", tag="lead%d" % turn, align_bytes=64, offset=turn * 4 * V)
+            gain = placed.tile([P, V], F32, name="gain", tag="gain%d" % turn, align_bytes=64, offset=GAIN_AT + turn * 4 * V)
             nc.gpsimd.tensor_tensor(lead[:], y, x, SUBTRACT)
             nc.scalar.activation(gain[:], lead[:], RELU)
             nc.gpsimd.tensor_tensor(dst, gain[:], x, ADD)
 
-        pair = [keep.tile([P, V], BF16, name="pair%d" % t, align_bytes=64) for t in range(PACK - 1)]
-        for t in range(PACK - 1):
-            nbr = [keep.tile([P, V], BF16, name="nbr", tag="nbr%d_%d" % (t, d), align_bytes=64) for d in range(2)]
-            for d in range(2):
-                fetch(nbr[d][:], pos_sb[d], t, 0, V)
-            larger_aside(pair[t][:], nbr[0][:], nbr[1][:])
-            if t < SIDE_PLANES:
-                third = keep.tile([P, V], BF16, name="third%d" % t, align_bytes=64)
-                fetch(third[:], pos_sb[2], t, 0, V)
-                larger_aside(top[:, t, :], pair[t][:], third[:])
+        pair = [keep.tile([P, V], BF16, name="pair0", align_bytes=64)]
+        pair.append(placed.tile([P, V], BF16, name="pair1", align_bytes=64, offset=BASE_AT))
+        pair.append(keep.tile([P, V], BF16, name="pair2", align_bytes=64))
+        nbr = [[keep.tile([P, V], BF16, name="nbr%d_%d" % (t, d), align_bytes=64) for d in range(3)] for t in range(SIDE_PLANES)]
+        nbr.append([placed.tile([P, V], BF16, name="nbr2_%d" % d, align_bytes=64, offset=BASE_AT + (d + 1) * 2 * V) for d in range(2)])
+        for t in range(PACK):
+            for d, dst in enumerate(nbr[t] if t < len(nbr) else ()):
+                fetch(dst[:], pos_sb[d], t, 0, V)
             fetch(own[:, t, :], cen_sb, t, 0, V)
-        fetch(own[:, PACK - 1, :], cen_sb, PACK - 1, 0, V)
-        last_turn = (len(steps) - 1) % 2
+        larger_aside(pair[0][:], nbr[0][0][:], nbr[0][1][:])
+        larger_aside(top[:, 0, :], pair[0][:], nbr[0][2][:])
+        larger_aside(pair[1][:], nbr[1][0][:], nbr[1][1][:])
+        larger_aside(pair[2][:], nbr[2][0][:], nbr[2][1][:])
+        larger_aside(top[:, 1, :], pair[1][:], nbr[1][2][:])
 
-        own_bf = keep.tile([P, V, PACK], BF16, name="own_bf", tag="lead%d" % last_turn, align_bytes=64)
+        own_bf = placed.tile([P, V, PACK], BF16, name="own_bf", align_bytes=64, offset=0)
         own_codes = keep.tile([P, V], U32, name="own_codes", align_bytes=64)
         own_scale = keep.tile([P, V], U8, name="own_scale", align_bytes=64)
         weave(own_bf[:], own[:])
 
         top_bf = {}
         for a, b in ((0, LAST), (LAST, V)):
-            late = keep.tile([P, PACK, b - a], BF16, name="late", tag="late" if a == 0 else "nbr%d_0" % (PACK - 2), align_bytes=64)
-            pair3 = keep.tile([P, b - a], BF16, name="pair3", tag="gain%d" % last_turn if a == 0 else "pair3", align_bytes=64)
+            if a == 0:
+                late = keep.tile([P, PACK, b - a], BF16, name="late0", align_bytes=64)
+                pair3 = placed.tile([P, b - a], BF16, name="pair3_0", align_bytes=64, offset=GAIN_AT + 4 * V - 64)
+            else:
+                late = placed.tile([P, PACK, b - a], BF16, name="late1", align_bytes=64, offset=BASE_AT + V)
+                pair3 = keep.tile([P, b - a], BF16, name="pair3_1", align_bytes=64)
             for d in range(2):
                 fetch(late[:, d, :], pos_sb[d], PACK - 1, a, b)
             for t in (PACK - 2, PACK - 1):
@@ -196,7 +204,7 @@ def tile_picked_sagecat_maxrelu_p_kernel(tc, x_words, x_scales, w1, w2, w3, offs
                     top_bf[lo] = keep.tile([P, hi - lo, PACK], BF16, name="top_bf%d" % lo, align_bytes=64)
                     weave(top_bf[lo][:], top[:, :, lo:hi])
 
-        w23_codes = keep.tile([P, 2 * N], U32, name="w23_codes", tag="gain%d" % last_turn, align_bytes=64)
+        w23_codes = placed.tile([P, 2 * N], U32, name="w23_codes", align_bytes=64, offset=GAIN_AT + 4 * V - 64)
         quantise(w23_codes[:], w23_scale[:], w23_bf[:])
         for a in range(0, V, V // 2):
             quantise(own_codes[:, a : a + V // 2], own_scale[:, a : a + V // 2], own_bf[:, a : a + V // 2, :])

@@ -29,6 +29,7 @@ SIDE_PLANES = 2
 LAST = 384
 GAIN_AT = 2 * 4 * V
 BASE_AT = 4 * 4 * V
+CODES_AT = BASE_AT + 3 * 2 * V
 CHUNKS = ((0, 256), (256, LAST), (LAST, V))
 
 
@@ -69,7 +70,7 @@ def tile_picked_sagecat_maxrelu_p_kernel(tc, x_words, x_scales, w1, w2, w3, offs
                 x_scale[first : first + QUADRANT // BLOCK_ROWS, :].bitcast(I32),
                 picked_scale[first : first + QUADRANT : BLOCK_ROWS, :].bitcast(I32),
             )
-        x_codes = [keep.tile([P, BANK], U32, name="x_codes%d" % u, align_bytes=64) for u in range(S // BANK)]
+        x_codes = [placed.tile([P, BANK], U32, name="x_codes%d" % u, align_bytes=64, offset=CODES_AT + u * 4 * BANK) for u in range(S // BANK)]
         for u in range(S // BANK):
             entries = offs_sb[:, u * BANK // PER_COLUMN : (u + 1) * BANK // PER_COLUMN]
             nc.vector.tensor_copy(x_codes[u][:], table_words[:].bitcast(U32).indirect(entries))
@@ -144,7 +145,7 @@ def tile_picked_sagecat_maxrelu_p_kernel(tc, x_words, x_scales, w1, w2, w3, offs
                 nc.sync.dma_start(w23_raw[:, t, e * N : (e + 1) * N], w.rearrange("(b t r) c -> t b r c", t=PACK, r=BLOCK_ROWS)[t])
         weave(w23_bf[:], w23_raw[:])
 
-        own = keep.tile([P, PACK, V], BF16, name="own", align_bytes=64)
+        own = placed.tile([P, PACK, V], BF16, name="own", align_bytes=64, offset=CODES_AT)
         top = keep.tile([P, PACK, V], BF16, name="top", tag="top", align_bytes=64)
 
         def fetch(dst, idx, t, a, b):
@@ -169,9 +170,10 @@ def tile_picked_sagecat_maxrelu_p_kernel(tc, x_words, x_scales, w1, w2, w3, offs
         pair.append(keep.tile([P, V], BF16, name="pair2", align_bytes=64))
         nbr = [[keep.tile([P, V], BF16, name="nbr%d_%d" % (t, d), align_bytes=64) for d in range(3)] for t in range(SIDE_PLANES)]
         nbr.append([placed.tile([P, V], BF16, name="nbr2_%d" % d, align_bytes=64, offset=BASE_AT + (d + 1) * 2 * V) for d in range(2)])
-        for t in range(PACK):
-            for d, dst in enumerate(nbr[t] if t < len(nbr) else ()):
+        for t, row in enumerate(nbr):
+            for d, dst in enumerate(row):
                 fetch(dst[:], pos_sb[d], t, 0, V)
+        for t in range(PACK):
             fetch(own[:, t, :], cen_sb, t, 0, V)
         larger_aside(pair[0][:], nbr[0][0][:], nbr[0][1][:])
         larger_aside(top[:, 0, :], pair[0][:], nbr[0][2][:])

@@ -30,6 +30,8 @@ LAST = 384
 GAIN_AT = 2 * 4 * V
 BASE_AT = 4 * 4 * V
 CODES_AT = BASE_AT + 3 * 2 * V
+H_AT = CODES_AT + 4 * S
+W23_AT = H_AT + 2 * 4 * S
 CHUNKS = ((0, 256), (256, LAST), (LAST, V))
 
 
@@ -79,7 +81,8 @@ def tile_picked_sagecat_maxrelu_p_kernel(tc, x_words, x_scales, w1, w2, w3, offs
         w1_bf = [keep.tile([P, hi - lo, P, PACK], BF16, name="w1_bf%d" % lo, tag="w1_bf%d" % lo, align_bytes=64) for lo, hi in groups]
         w1_codes = [keep.tile([P, hi - lo, P], U32, name="w1_codes%d" % lo, tag="w1_codes" if lo == 0 else "w1_bf0", align_bytes=64) for lo, hi in groups]
         w1_scale = keep.tile([P, PACK, P], U8, name="w1_scale", align_bytes=64)
-        h = [keep.tile([P, S], F32, name="h%d" % t, align_bytes=64) for t in range(PACK)]
+        h = [keep.tile([P, S], F32, name="h%d" % t, align_bytes=64) for t in range(2)]
+        h.extend(placed.tile([P, S], F32, name="h%d" % t, align_bytes=64, offset=H_AT + (t - 2) * 4 * S) for t in range(2, PACK))
 
         def quantise(codes, scale, woven):
             nc.vector.quantize_mx(out=codes.bitcast(FP8X4), scales=scale, in_=woven.rearrange("p c j -> p (c j)"))
@@ -120,10 +123,14 @@ def tile_picked_sagecat_maxrelu_p_kernel(tc, x_words, x_scales, w1, w2, w3, offs
                 start=True,
                 stop=True,
             )
-            if t == 0 and b == S:
-                nc.vector.tensor_scalar_max(h[t][:, a:b], acc[:], 0.0)
-            else:
-                nc.scalar.activation(h[t][:, a:b], acc[:], RELU)
+            return acc
+
+        def empty(t):
+            for (a, b), acc in products[t]:
+                if t == 0 and b == S:
+                    nc.vector.tensor_scalar_max(h[t][:, a:b], acc[:], 0.0)
+                else:
+                    nc.scalar.activation(h[t][:, a:b], acc[:], RELU)
 
         round_w1(nc.scalar.copy, 0, 0, 2)
         round_w1(nc.vector.tensor_copy, 0, 2, PACK)
@@ -132,18 +139,19 @@ def tile_picked_sagecat_maxrelu_p_kernel(tc, x_words, x_scales, w1, w2, w3, offs
         quantise_w1(0, 0, 1)
         quantise_w1(1, 1, 2)
         quantise_w1(1, 2, PACK)
+        products = []
         for t in range(PACK):
             width = BANK // 2 if t == 0 else BANK
-            for a in range(0, S, width):
-                first_product(t, a, a + width)
+            products.append([((a, a + width), first_product(t, a, a + width)) for a in range(0, S, width)])
+            if t < 2:
+                empty(t)
 
-        w23_bf = keep.tile([P, 2 * N, PACK], BF16, name="w23_bf", align_bytes=64)
+        w23_bf = placed.tile([P, 2 * N, PACK], BF16, name="w23_bf", align_bytes=64, offset=W23_AT)
         w23_scale = keep.tile([P, 2 * N], U8, name="w23_scale", align_bytes=64)
         w23_raw = keep.tile([P, PACK, 2 * N], F32, name="w23_raw", tag="raw", align_bytes=64)
         for e, w in enumerate((w2, w3)):
             for t in range(PACK):
                 nc.sync.dma_start(w23_raw[:, t, e * N : (e + 1) * N], w.rearrange("(b t r) c -> t b r c", t=PACK, r=BLOCK_ROWS)[t])
-        weave(w23_bf[:], w23_raw[:])
 
         own = placed.tile([P, PACK, V], BF16, name="own", align_bytes=64, offset=CODES_AT)
         top = keep.tile([P, PACK, V], BF16, name="top", tag="top", align_bytes=64)
@@ -156,11 +164,12 @@ def tile_picked_sagecat_maxrelu_p_kernel(tc, x_words, x_scales, w1, w2, w3, offs
 
         steps = []
 
-        def larger_aside(dst, x, y):
+        def larger_aside(dst, x, y, gain_at):
             turn = len(steps) % 2
             steps.append(dst)
-            lead = placed.tile([P, V], F32, name="lead", tag="lead%d" % turn, align_bytes=64, offset=turn * 4 * V)
-            gain = placed.tile([P, V], F32, name="gain", tag="gain%d" % turn, align_bytes=64, offset=GAIN_AT + turn * 4 * V)
+            width = dst.shape[1]
+            lead = placed.tile([P, width], F32, name="lead", tag="lead%d" % turn, align_bytes=64, offset=turn * 4 * V)
+            gain = placed.tile([P, width], F32, name="gain", tag="gain%d" % len(steps), align_bytes=64, offset=gain_at)
             nc.gpsimd.tensor_tensor(lead[:], y, x, SUBTRACT)
             nc.scalar.activation(gain[:], lead[:], RELU)
             nc.gpsimd.tensor_tensor(dst, gain[:], x, ADD)
@@ -168,18 +177,28 @@ def tile_picked_sagecat_maxrelu_p_kernel(tc, x_words, x_scales, w1, w2, w3, offs
         pair = [keep.tile([P, V], BF16, name="pair0", align_bytes=64)]
         pair.append(placed.tile([P, V], BF16, name="pair1", align_bytes=64, offset=BASE_AT))
         pair.append(keep.tile([P, V], BF16, name="pair2", align_bytes=64))
-        nbr = [[keep.tile([P, V], BF16, name="nbr%d_%d" % (t, d), align_bytes=64) for d in range(3)] for t in range(SIDE_PLANES)]
+        nbr = [[keep.tile([P, V], BF16, name="nbr%d_%d" % (t, d), align_bytes=64) for d in range(2)] for t in range(SIDE_PLANES)]
+        nbr[0].append(keep.tile([P, V], BF16, name="nbr0_2", tag="w1_bf0", align_bytes=64))
+        nbr[1].append(keep.tile([P, V], BF16, name="nbr1_2", align_bytes=64))
         nbr.append([placed.tile([P, V], BF16, name="nbr2_%d" % d, align_bytes=64, offset=BASE_AT + (d + 1) * 2 * V) for d in range(2)])
-        for t, row in enumerate(nbr):
-            for d, dst in enumerate(row):
-                fetch(dst[:], pos_sb[d], t, 0, V)
+        halves = ((0, V // 2), (V // 2, V))
+        for u, (a, b) in enumerate(halves):
+            for d in range(2):
+                fetch(nbr[0][d][:, a:b], pos_sb[d], 0, a, b)
+            larger_aside(pair[0][:, a:b], nbr[0][0][:, a:b], nbr[0][1][:, a:b], H_AT + u * 4 * S)
+        for t, d in ((1, 0), (1, 1), (0, 2), (1, 2)):
+            fetch(nbr[t][d][:], pos_sb[d], t, 0, V)
+        larger_aside(pair[1][:], nbr[1][0][:], nbr[1][1][:], W23_AT)
+        empty(2)
+        empty(3)
+        for d in range(2):
+            fetch(nbr[2][d][:], pos_sb[d], 2, 0, V)
         for t in range(PACK):
             fetch(own[:, t, :], cen_sb, t, 0, V)
-        larger_aside(pair[0][:], nbr[0][0][:], nbr[0][1][:])
-        larger_aside(top[:, 0, :], pair[0][:], nbr[0][2][:])
-        larger_aside(pair[1][:], nbr[1][0][:], nbr[1][1][:])
-        larger_aside(pair[2][:], nbr[2][0][:], nbr[2][1][:])
-        larger_aside(top[:, 1, :], pair[1][:], nbr[1][2][:])
+        larger_aside(top[:, 0, :], pair[0][:], nbr[0][2][:], GAIN_AT)
+        larger_aside(top[:, 1, :], pair[1][:], nbr[1][2][:], GAIN_AT + 4 * V)
+        larger_aside(pair[2][:], nbr[2][0][:], nbr[2][1][:], GAIN_AT)
+        weave(w23_bf[:], w23_raw[:])
 
         own_bf = placed.tile([P, V, PACK], BF16, name="own_bf", align_bytes=64, offset=0)
         own_codes = keep.tile([P, V], U32, name="own_codes", align_bytes=64)

@@ -50,20 +50,20 @@ def tile_picked_sagecat_maxrelu_p_kernel(tc, x_words, x_scales, w1, w2, w3, offs
         x_scale = keep.tile([P, S], U8, name="x_scale", align_bytes=64)
         w1_raw = keep.tile([P, PACK, H], F32, name="w1_raw", tag="raw", align_bytes=64)
 
-        nc.vector.memset(table_scales[:].bitcast(I32), 0)
+        nc.vector.memset(table_scales[:, : T // 2].bitcast(I32), 0)
+        nc.gpsimd.memset(table_scales[:, T // 2 :].bitcast(I32), 0)
         nc.vector.memset(x_scale[:].bitcast(I32), 0)
         words_hbm = x_words[0].rearrange("p c r -> p (c r)").bitcast(I32)
         w1_rows = w1.rearrange("(p j) c -> p j c", j=PACK)
         nc.sync.dma_start(table_words[:, :HEAD_COLS], words_hbm[:, :HEAD_COLS])
         nc.sync.dma_start(offs_sb[:], offs)
         nc.sync.dma_start(cen_sb[:], cen)
-        nc.sync.dma_start(pos_sb[0][:], pos1)
-        nc.sync.dma_start(pos_sb[1][:], pos2)
         nc.sync.dma_start(table_scales[0:P:BLOCK_ROWS, :].bitcast(I32), x_scales[0].bitcast(I32))
         nc.sync.dma_start(table_words[:, HEAD_COLS:], words_hbm[:, HEAD_COLS:])
         for e in range(2):
             nc.sync.dma_start(w1_raw[:, 2 * e : 2 * e + 2, :], w1_rows[:, 2 * e : 2 * e + 2, :])
-        nc.sync.dma_start(pos_sb[2][:], pos3)
+        for tile, pos in zip(pos_sb, (pos1, pos2, pos3)):
+            nc.sync.dma_start(tile[:], pos)
 
         picked_scale = keep.tile([P, S], U8, name="picked_scale", align_bytes=64)
         nc.vector.tensor_copy(picked_scale[:], table_scales[:].indirect(offs_sb[:]))
@@ -90,9 +90,9 @@ def tile_picked_sagecat_maxrelu_p_kernel(tc, x_words, x_scales, w1, w2, w3, offs
         def weave(dst, src):
             nc.scalar.copy(dst.rearrange("p (c i) j -> p c j i", i=4), src.rearrange("p j (c i) -> p c j i", i=4))
 
-        def round_w1(copy, g, j0, j1):
-            lo, hi = groups[g]
-            dst = w1_bf[g][:, :, :, j0:j1].rearrange("p t (b r) j -> p t b r j", r=BLOCK_ROWS)
+        def round_w1(copy, g, lo, hi, j0, j1):
+            first = groups[g][0]
+            dst = w1_bf[g][:, lo - first : hi - first, :, j0:j1].rearrange("p t (b r) j -> p t b r j", r=BLOCK_ROWS)
             src = w1_raw[:, j0:j1, :].rearrange("p j (b t r) -> p t b r j", t=PACK, r=BLOCK_ROWS)[:, lo:hi]
             copy(dst, src)
 
@@ -113,16 +113,17 @@ def tile_picked_sagecat_maxrelu_p_kernel(tc, x_words, x_scales, w1, w2, w3, offs
 
         def first_product(t, a, b):
             acc = next_bank(b - a, "acc")
-            u, c = divmod(a, BANK)
-            nc.tensor.matmul_mx(
-                out=acc[:],
-                lhsT=w1_codes[min(t, 1)][:, max(t - 1, 0), :].bitcast(FP8X4),
-                lhsT_scale=w1_scale[:, t, :],
-                rhs=x_codes[u][:, c : c + b - a].bitcast(FP8X4),
-                rhs_scale=x_scale[:, a:b],
-                start=True,
-                stop=True,
-            )
+            for lo in range(a, b, BANK // 2):
+                u, c = divmod(lo, BANK)
+                nc.tensor.matmul_mx(
+                    out=acc[:, lo - a : lo - a + BANK // 2],
+                    lhsT=w1_codes[min(t, 1)][:, max(t - 1, 0), :].bitcast(FP8X4),
+                    lhsT_scale=w1_scale[:, t, :],
+                    rhs=x_codes[u][:, c : c + BANK // 2].bitcast(FP8X4),
+                    rhs_scale=x_scale[:, lo : lo + BANK // 2],
+                    start=True,
+                    stop=True,
+                )
             return acc
 
         def empty(t):
@@ -132,10 +133,23 @@ def tile_picked_sagecat_maxrelu_p_kernel(tc, x_words, x_scales, w1, w2, w3, offs
                 else:
                     nc.scalar.activation(h[t][:, a:b], acc[:], RELU)
 
-        round_w1(nc.scalar.copy, 0, 0, 2)
-        round_w1(nc.vector.tensor_copy, 0, 2, PACK)
-        round_w1(nc.scalar.copy, 1, 0, 2)
-        round_w1(nc.scalar.copy, 1, 2, PACK)
+        idle = psum.tile([P, BANK], F32, name="idle", tag="bank%d" % (BANKS - 1))
+        for u in range(2):
+            nc.tensor.matmul_mx(
+                out=idle[:],
+                lhsT=x_codes[0][:, :P].bitcast(FP8X4),
+                lhsT_scale=picked_scale[:, :P],
+                rhs=x_codes[0][:].bitcast(FP8X4),
+                rhs_scale=picked_scale[:, :BANK],
+                start=True,
+                stop=True,
+            )
+
+        round_w1(nc.scalar.copy, 0, 0, 1, 0, 2)
+        round_w1(nc.vector.tensor_copy, 0, 0, 1, 2, PACK)
+        round_w1(nc.scalar.copy, 1, 1, PACK, 0, 2)
+        round_w1(nc.vector.tensor_copy, 1, 1, 2, 2, PACK)
+        round_w1(nc.scalar.copy, 1, 2, PACK, 2, PACK)
         quantise_w1(0, 0, 1)
         quantise_w1(1, 1, 2)
         quantise_w1(1, 2, PACK)

@@ -14,6 +14,7 @@ U8 = mybir.dt.uint8
 FP8X4 = mybir.dt.float8_e4m3fn_x4
 MAX = mybir.AluOpType.max
 ADD = mybir.AluOpType.add
+MULT = mybir.AluOpType.mult
 SUBTRACT = mybir.AluOpType.subtract
 RELU = mybir.ActivationFunctionType.Relu
 
@@ -96,6 +97,9 @@ def tile_picked_sagecat_maxrelu_p_kernel(tc, x_words, x_scales, w1, w2, w3, offs
             src = w1_raw[:, j0:j1, :].rearrange("p j (b t r) -> p t b r j", t=PACK, r=BLOCK_ROWS)[:, lo:hi]
             copy(dst, src)
 
+        def round_aside(dst, src):
+            nc.gpsimd.tensor_scalar(dst[:, 0], src[:, 0], 1.0, 0.0, MULT, ADD)
+
         def quantise_w1(g, lo, hi):
             first = groups[g][0]
             quantise(
@@ -147,7 +151,8 @@ def tile_picked_sagecat_maxrelu_p_kernel(tc, x_words, x_scales, w1, w2, w3, offs
 
         round_w1(nc.scalar.copy, 0, 0, 1, 0, 2)
         round_w1(nc.vector.tensor_copy, 0, 0, 1, 2, PACK)
-        round_w1(nc.scalar.copy, 1, 1, PACK, 0, 2)
+        round_w1(nc.scalar.copy, 1, 1, PACK - 1, 0, 2)
+        round_w1(round_aside, 1, PACK - 1, PACK, 0, 2)
         round_w1(nc.vector.tensor_copy, 1, 1, 2, 2, PACK)
         round_w1(nc.scalar.copy, 1, 2, PACK, 2, PACK)
         quantise_w1(0, 0, 1)

@@ -1,6 +1,7 @@
 from contextlib import ExitStack
 
 import concourse.mybir as mybir
+from concourse.masks import make_identity
 
 K, T, S, V, H, N = 512, 4096, 1024, 512, 512, 128
 FLOPS = 2 * K * H * S + 2 * 2 * H * N * V
@@ -12,7 +13,6 @@ U32 = mybir.dt.uint32
 U16 = mybir.dt.uint16
 U8 = mybir.dt.uint8
 FP8X4 = mybir.dt.float8_e4m3fn_x4
-MAX = mybir.AluOpType.max
 ADD = mybir.AluOpType.add
 MULT = mybir.AluOpType.mult
 SUBTRACT = mybir.AluOpType.subtract
@@ -26,21 +26,14 @@ PER_COLUMN = 16
 BANK = 512
 BANKS = 8
 HEAD_COLS = 1024
-SIDE_PLANES = 2
-LAST = 384
-GAIN_AT = 2 * 4 * V
-BASE_AT = 4 * 4 * V
-CODES_AT = BASE_AT + 3 * 2 * V
-H_AT = CODES_AT + 4 * S
-W23_AT = H_AT + 2 * 4 * S
-CHUNKS = ((0, 256), (256, LAST), (LAST, V))
+HALF = V // 2
+CHUNKS = ((0, HALF), (HALF, HALF + P), (HALF + P, V))
 
 
 def tile_picked_sagecat_maxrelu_p_kernel(tc, x_words, x_scales, w1, w2, w3, offs, cen, pos1, pos2, pos3, out):
     nc = tc.nc
     with ExitStack() as ctx:
         keep = ctx.enter_context(tc.tile_pool(name="keep", bufs=1))
-        placed = ctx.enter_context(tc.tile_pool(name="placed", bufs=1))
         psum = ctx.enter_context(tc.psum_pool(name="psum", bufs=1))
 
         offs_sb = keep.tile([P, S // PER_COLUMN], U16, name="offs_sb")
@@ -54,6 +47,8 @@ def tile_picked_sagecat_maxrelu_p_kernel(tc, x_words, x_scales, w1, w2, w3, offs
         nc.vector.memset(table_scales[:, : T // 2].bitcast(I32), 0)
         nc.gpsimd.memset(table_scales[:, T // 2 :].bitcast(I32), 0)
         nc.vector.memset(x_scale[:].bitcast(I32), 0)
+        identity = keep.tile([P, P], F32, name="identity", align_bytes=64)
+        make_identity(nc, identity[:])
         words_hbm = x_words[0].rearrange("p c r -> p (c r)").bitcast(I32)
         w1_rows = w1.rearrange("(p j) c -> p j c", j=PACK)
         nc.sync.dma_start(table_words[:, :HEAD_COLS], words_hbm[:, :HEAD_COLS])
@@ -73,7 +68,7 @@ def tile_picked_sagecat_maxrelu_p_kernel(tc, x_words, x_scales, w1, w2, w3, offs
                 x_scale[first : first + QUADRANT // BLOCK_ROWS, :].bitcast(I32),
                 picked_scale[first : first + QUADRANT : BLOCK_ROWS, :].bitcast(I32),
             )
-        x_codes = [placed.tile([P, BANK], U32, name="x_codes%d" % u, align_bytes=64, offset=CODES_AT + u * 4 * BANK) for u in range(S // BANK)]
+        x_codes = [keep.tile([P, BANK], U32, name="x_codes%d" % u, align_bytes=64) for u in range(S // BANK)]
         for u in range(S // BANK):
             entries = offs_sb[:, u * BANK // PER_COLUMN : (u + 1) * BANK // PER_COLUMN]
             nc.vector.tensor_copy(x_codes[u][:], table_words[:].bitcast(U32).indirect(entries))
@@ -82,8 +77,7 @@ def tile_picked_sagecat_maxrelu_p_kernel(tc, x_words, x_scales, w1, w2, w3, offs
         w1_bf = [keep.tile([P, hi - lo, P, PACK], BF16, name="w1_bf%d" % lo, tag="w1_bf%d" % lo, align_bytes=64) for lo, hi in groups]
         w1_codes = [keep.tile([P, hi - lo, P], U32, name="w1_codes%d" % lo, tag="w1_codes" if lo == 0 else "w1_bf0", align_bytes=64) for lo, hi in groups]
         w1_scale = keep.tile([P, PACK, P], U8, name="w1_scale", align_bytes=64)
-        h = [keep.tile([P, S], F32, name="h%d" % t, align_bytes=64) for t in range(2)]
-        h.extend(placed.tile([P, S], F32, name="h%d" % t, align_bytes=64, offset=H_AT + (t - 2) * 4 * S) for t in range(2, PACK))
+        h = [keep.tile([P, S], F32, name="h%d" % t, align_bytes=64) for t in range(PACK)]
 
         def quantise(codes, scale, woven):
             nc.vector.quantize_mx(out=codes.bitcast(FP8X4), scales=scale, in_=woven.rearrange("p c j -> p (c j)"))
@@ -162,121 +156,103 @@ def tile_picked_sagecat_maxrelu_p_kernel(tc, x_words, x_scales, w1, w2, w3, offs
         for t in range(PACK):
             width = BANK // 2 if t == 0 else BANK
             products.append([((a, a + width), first_product(t, a, a + width)) for a in range(0, S, width)])
-            if t < 2:
-                empty(t)
+            empty(t)
 
-        w23_bf = placed.tile([P, 2 * N, PACK], BF16, name="w23_bf", align_bytes=64, offset=W23_AT)
+        w23_bf = keep.tile([P, 2 * N, PACK], BF16, name="w23_bf", align_bytes=64)
         w23_scale = keep.tile([P, 2 * N], U8, name="w23_scale", align_bytes=64)
         w23_raw = keep.tile([P, PACK, 2 * N], F32, name="w23_raw", tag="raw", align_bytes=64)
         for e, w in enumerate((w2, w3)):
             for t in range(PACK):
                 nc.sync.dma_start(w23_raw[:, t, e * N : (e + 1) * N], w.rearrange("(b t r) c -> t b r c", t=PACK, r=BLOCK_ROWS)[t])
-
-        own = placed.tile([P, PACK, V], BF16, name="own", align_bytes=64, offset=CODES_AT)
-        top = keep.tile([P, PACK, V], BF16, name="top", tag="top", align_bytes=64)
+        weave(w23_bf[:], w23_raw[:])
 
         def fetch(dst, idx, t, a, b):
             nc.vector.tensor_copy(dst, h[t][:].indirect(idx[:, a // PER_COLUMN : b // PER_COLUMN]))
 
-        def larger(dst, x, y):
-            nc.vector.tensor_tensor(dst, x, y, MAX)
+        def plane_tile(name, t):
+            return keep.tile([P, V], F32, name="%s%d" % (name, t), align_bytes=64)
 
-        steps = []
+        def turn(dst, term, start, stop):
+            nc.tensor.matmul(dst, term, identity[:], start=start, stop=stop, is_transpose=True)
 
-        def larger_aside(dst, x, y, gain_at):
-            turn = len(steps) % 2
-            steps.append(dst)
-            width = dst.shape[1]
-            lead = placed.tile([P, width], F32, name="lead", tag="lead%d" % turn, align_bytes=64, offset=turn * 4 * V)
-            gain = placed.tile([P, width], F32, name="gain", tag="gain%d" % len(steps), align_bytes=64, offset=gain_at)
+        def columns(u):
+            return slice(u * P, (u + 1) * P)
+
+        top = [psum.tile([P, PACK, P], F32, name="top%d" % u, tag="bank%d" % (PACK + u)) for u in range(V // P)]
+        nbr = [[plane_tile("nbr%d_" % d, t) for d in range(3)] for t in range(PACK)]
+        for t in range(PACK - 1):
+            for d in range(3):
+                fetch(nbr[t][d][:], pos_sb[d], t, 0, V)
+        for d, a in ((0, 0), (1, 0), (0, HALF), (2, 0), (1, HALF), (2, HALF)):
+            fetch(nbr[PACK - 1][d][:, a : a + HALF], pos_sb[d], PACK - 1, a, a + HALF)
+        steps = [(t, 0, V) for t in range(PACK - 1)] + [(PACK - 1, 0, HALF), (PACK - 1, HALF, V)]
+        for n, (t, a, b) in enumerate(steps):
+            x, y, z = (nbr[t][d][:, a:b] for d in range(3))
+            tiles = range((b - a) // P)
+            lead, rest, third, extra = (
+                keep.tile([P, b - a], F32, name="%s%d" % (name, n), align_bytes=64) for name in ("lead", "rest", "third", "extra")
+            )
+            gain = keep.tile([P, b - a], F32, name="gain", tag="rest%d" % (n - 1), align_bytes=64)
             nc.gpsimd.tensor_tensor(lead[:], y, x, SUBTRACT)
             nc.scalar.activation(gain[:], lead[:], RELU)
-            nc.gpsimd.tensor_tensor(dst, gain[:], x, ADD)
+            turned = psum.tile([P, b - a], F32, name="turned", tag="bank%d" % (n % 2))
+            for u in tiles:
+                turn(turned[:, columns(u)], z[:, columns(u)], True, True)
+            nc.scalar.copy(third[:], turned[:])
+            nc.gpsimd.tensor_tensor(rest[:], x, z, SUBTRACT)
+            margin = psum.tile([P, b - a], F32, name="margin", tag="bank%d" % ((n + 1) % 2))
+            for term in (gain, rest):
+                for u in tiles:
+                    turn(margin[:, columns(u)], term[:, columns(u)], term is gain and u == 0, term is rest and u == tiles[-1])
+            nc.scalar.activation(extra[:], margin[:], RELU)
+            for term, opens in ((third, True), (extra, False)):
+                for u in tiles:
+                    turn(top[a // P + u][:, t, :], term[:, columns(u)], opens, not opens)
 
-        pair = [keep.tile([P, V], BF16, name="pair0", align_bytes=64)]
-        pair.append(placed.tile([P, V], BF16, name="pair1", align_bytes=64, offset=BASE_AT))
-        pair.append(keep.tile([P, V], BF16, name="pair2", align_bytes=64))
-        nbr = [[keep.tile([P, V], BF16, name="nbr%d_%d" % (t, d), align_bytes=64) for d in range(2)] for t in range(SIDE_PLANES)]
-        nbr[0].append(keep.tile([P, V], BF16, name="nbr0_2", tag="w1_bf0", align_bytes=64))
-        nbr[1].append(keep.tile([P, V], BF16, name="nbr1_2", align_bytes=64))
-        nbr.append([placed.tile([P, V], BF16, name="nbr2_%d" % d, align_bytes=64, offset=BASE_AT + (d + 1) * 2 * V) for d in range(2)])
-        halves = ((0, V // 2), (V // 2, V))
-        for u, (a, b) in enumerate(halves):
-            for d in range(2):
-                fetch(nbr[0][d][:, a:b], pos_sb[d], 0, a, b)
-            larger_aside(pair[0][:, a:b], nbr[0][0][:, a:b], nbr[0][1][:, a:b], H_AT + u * 4 * S)
-        for t, d in ((1, 0), (1, 1), (0, 2), (1, 2)):
-            fetch(nbr[t][d][:], pos_sb[d], t, 0, V)
-        larger_aside(pair[1][:], nbr[1][0][:], nbr[1][1][:], W23_AT)
-        empty(2)
-        empty(3)
-        for d in range(2):
-            fetch(nbr[2][d][:], pos_sb[d], 2, 0, V)
-        for t in range(PACK):
-            fetch(own[:, t, :], cen_sb, t, 0, V)
-        larger_aside(top[:, 0, :], pair[0][:], nbr[0][2][:], GAIN_AT)
-        larger_aside(top[:, 1, :], pair[1][:], nbr[1][2][:], GAIN_AT + 4 * V)
-        larger_aside(pair[2][:], nbr[2][0][:], nbr[2][1][:], GAIN_AT)
-        weave(w23_bf[:], w23_raw[:])
+        top_bf = keep.tile([P, V, PACK], BF16, name="top_bf", align_bytes=64)
+        for u in range(V // P):
+            nc.scalar.copy(top_bf[:, columns(u), :], top[u][:].rearrange("p t v -> p v t"))
 
-        own_bf = placed.tile([P, V, PACK], BF16, name="own_bf", align_bytes=64, offset=0)
+        own = []
+        for u in range(2):
+            own.append(keep.tile([P, PACK, HALF], BF16, name="own%d" % u, tag="nbr%d_%d" % (1 - u, PACK - 2), align_bytes=64))
+            for t in range(PACK):
+                fetch(own[u][:, t, :], cen_sb, t, u * HALF, (u + 1) * HALF)
+        own_bf = [keep.tile([P, HALF, PACK], BF16, name="own_bf0", align_bytes=64)]
+        nc.gpsimd.tensor_scalar(own_bf[0][:], own[0][:].rearrange("p t v -> p v t"), 1.0, 0.0, MULT, ADD)
+        own_bf.append(keep.tile([P, HALF, PACK], BF16, name="own_bf1", tag="extra%d" % PACK, align_bytes=64))
+        for u in range(2):
+            weave(own_bf[1][:, columns(u), :], own[1][:, :, columns(u)])
+
+        w23_codes = keep.tile([P, 2 * N], U32, name="w23_codes", tag="nbr1_%d" % (PACK - 2), align_bytes=64)
+        quantise(w23_codes[:], w23_scale[:], w23_bf[:])
         own_codes = keep.tile([P, V], U32, name="own_codes", align_bytes=64)
         own_scale = keep.tile([P, V], U8, name="own_scale", align_bytes=64)
-        weave(own_bf[:], own[:])
+        top_codes = keep.tile([P, V], U32, name="top_codes", align_bytes=64)
+        top_scale = keep.tile([P, V], U8, name="top_scale", align_bytes=64)
+        quantise(own_codes[:, :HALF], own_scale[:, :HALF], own_bf[0][:])
+        for a in range(0, V, HALF):
+            quantise(top_codes[:, a : a + HALF], top_scale[:, a : a + HALF], top_bf[:, a : a + HALF, :])
+        for a, b in CHUNKS[1:]:
+            quantise(own_codes[:, a:b], own_scale[:, a:b], own_bf[1][:, a - HALF : b - HALF, :])
 
-        top_bf = {}
-        for a, b in ((0, LAST), (LAST, V)):
-            if a == 0:
-                late = keep.tile([P, PACK, b - a], BF16, name="late0", align_bytes=64)
-                pair3 = placed.tile([P, b - a], BF16, name="pair3_0", align_bytes=64, offset=GAIN_AT + 4 * V - 64)
+        early = keep.tile([P, HALF], F32, name="early", align_bytes=64)
+        ending = keep.tile([P, HALF], F32, name="ending", align_bytes=64)
+        for n, (a, b) in enumerate(CHUNKS):
+            acc = psum.tile([P, b - a], F32, name="sum%d" % a, tag="bank%d" % n)
+            for e, (codes, scale) in ((1, (top_codes, top_scale)), (0, (own_codes, own_scale))):
+                nc.tensor.matmul_mx(
+                    out=acc[:],
+                    lhsT=w23_codes[:, e * N : (e + 1) * N].bitcast(FP8X4),
+                    lhsT_scale=w23_scale[:, e * N : (e + 1) * N],
+                    rhs=codes[:, a:b].bitcast(FP8X4),
+                    rhs_scale=scale[:, a:b],
+                    start=e == 1,
+                    stop=e == 0,
+                )
+            if n == 0:
+                nc.scalar.activation(early[:], acc[:], RELU)
+                nc.scalar.dma_start(out[:, :HALF], early[:])
             else:
-                late = placed.tile([P, PACK, b - a], BF16, name="late1", align_bytes=64, offset=BASE_AT + V)
-                pair3 = keep.tile([P, b - a], BF16, name="pair3_1", align_bytes=64)
-            for d in range(2):
-                fetch(late[:, d, :], pos_sb[d], PACK - 1, a, b)
-            for t in (PACK - 2, PACK - 1):
-                fetch(late[:, t, :], pos_sb[2], t, a, b)
-            larger(pair3[:], late[:, 0, :], late[:, 1, :])
-            larger(top[:, PACK - 2, a:b], pair[PACK - 2][:, a:b], late[:, PACK - 2, :])
-            larger(top[:, PACK - 1, a:b], pair3[:], late[:, PACK - 1, :])
-            for lo, hi in CHUNKS:
-                if a <= lo < b:
-                    top_bf[lo] = keep.tile([P, hi - lo, PACK], BF16, name="top_bf%d" % lo, align_bytes=64)
-                    weave(top_bf[lo][:], top[:, :, lo:hi])
-
-        w23_codes = placed.tile([P, 2 * N], U32, name="w23_codes", align_bytes=64, offset=GAIN_AT + 4 * V - 64)
-        quantise(w23_codes[:], w23_scale[:], w23_bf[:])
-        for a in range(0, V, V // 2):
-            quantise(own_codes[:, a : a + V // 2], own_scale[:, a : a + V // 2], own_bf[:, a : a + V // 2, :])
-        sums = {}
-        for a, b in CHUNKS:
-            sums[a] = next_bank(b - a, "sum%d" % a)
-            nc.tensor.matmul_mx(
-                out=sums[a][:],
-                lhsT=w23_codes[:, :N].bitcast(FP8X4),
-                lhsT_scale=w23_scale[:, :N],
-                rhs=own_codes[:, a:b].bitcast(FP8X4),
-                rhs_scale=own_scale[:, a:b],
-                start=True,
-                stop=False,
-            )
-        early = keep.tile([P, LAST], F32, name="early", tag="top", align_bytes=64)
-        ending = keep.tile([P, V - LAST], F32, name="ending", align_bytes=64)
-        for a, b in CHUNKS:
-            codes = keep.tile([P, b - a], U32, name="top_codes%d" % a, align_bytes=64)
-            scale = keep.tile([P, b - a], U8, name="top_scale%d" % a, align_bytes=64)
-            quantise(codes[:], scale[:], top_bf[a][:])
-            nc.tensor.matmul_mx(
-                out=sums[a][:],
-                lhsT=w23_codes[:, N:].bitcast(FP8X4),
-                lhsT_scale=w23_scale[:, N:],
-                rhs=codes[:].bitcast(FP8X4),
-                rhs_scale=scale[:],
-                start=False,
-                stop=True,
-            )
-        for a, b in CHUNKS[:-1]:
-            nc.scalar.activation(early[:, a:b], sums[a][:], RELU)
-        nc.scalar.dma_start(out[:, :LAST], early[:])
-        nc.vector.tensor_scalar_max(ending[:], sums[LAST][:], 0.0)
-        nc.sync.dma_start(out[:, LAST:], ending[:])
+                nc.vector.tensor_scalar_max(ending[:, a - HALF : b - HALF], acc[:], 0.0)
+        nc.sync.dma_start(out[:, HALF:], ending[:])

@@ -183,7 +183,7 @@ def tile_picked_sagecat_maxrelu_p_kernel(tc, x_words, x_scales, w1, w2, w3, offs
         for t in range(PACK - 1):
             for d in range(3):
                 fetch(nbr[t][d][:], pos_sb[d], t, 0, V)
-        for d, a in ((0, 0), (1, 0), (0, HALF), (2, 0), (1, HALF), (2, HALF)):
+        for a, d in ((a, d) for a in (0, HALF) for d in range(3)):
             fetch(nbr[PACK - 1][d][:, a : a + HALF], pos_sb[d], PACK - 1, a, a + HALF)
         steps = [(t, 0, V) for t in range(PACK - 1)] + [(PACK - 1, 0, HALF), (PACK - 1, HALF, V)]
         for n, (t, a, b) in enumerate(steps):
@@ -195,12 +195,12 @@ def tile_picked_sagecat_maxrelu_p_kernel(tc, x_words, x_scales, w1, w2, w3, offs
             gain = keep.tile([P, b - a], F32, name="gain", tag="rest%d" % (n - 1), align_bytes=64)
             nc.gpsimd.tensor_tensor(lead[:], y, x, SUBTRACT)
             nc.scalar.activation(gain[:], lead[:], RELU)
-            turned = psum.tile([P, b - a], F32, name="turned", tag="bank%d" % (n % 2))
+            turned = psum.tile([P, b - a], F32, name="turned", tag="bank%d" % (min(n, PACK - 1) % 2))
             for u in tiles:
                 turn(turned[:, columns(u)], z[:, columns(u)], True, True)
             nc.scalar.copy(third[:], turned[:])
             nc.gpsimd.tensor_tensor(rest[:], x, z, SUBTRACT)
-            margin = psum.tile([P, b - a], F32, name="margin", tag="bank%d" % ((n + 1) % 2))
+            margin = psum.tile([P, b - a], F32, name="margin", tag="bank%d" % ((n + 1) % 2 if n < PACK else 2))
             for term in (gain, rest):
                 for u in tiles:
                     turn(margin[:, columns(u)], term[:, columns(u)], term is gain and u == 0, term is rest and u == tiles[-1])
@@ -236,8 +236,9 @@ def tile_picked_sagecat_maxrelu_p_kernel(tc, x_words, x_scales, w1, w2, w3, offs
         for a, b in CHUNKS[1:]:
             quantise(own_codes[:, a:b], own_scale[:, a:b], own_bf[1][:, a - HALF : b - HALF, :])
 
-        early = keep.tile([P, HALF], F32, name="early", align_bytes=64)
-        ending = keep.tile([P, HALF], F32, name="ending", align_bytes=64)
+        last = CHUNKS[-1][0]
+        early = keep.tile([P, last], F32, name="early", align_bytes=64)
+        ending = keep.tile([P, V - last], F32, name="ending", align_bytes=64)
         for n, (a, b) in enumerate(CHUNKS):
             acc = psum.tile([P, b - a], F32, name="sum%d" % a, tag="bank%d" % n)
             for e, (codes, scale) in ((1, (top_codes, top_scale)), (0, (own_codes, own_scale))):
@@ -250,9 +251,8 @@ def tile_picked_sagecat_maxrelu_p_kernel(tc, x_words, x_scales, w1, w2, w3, offs
                     start=e == 1,
                     stop=e == 0,
                 )
-            if n == 0:
-                nc.scalar.activation(early[:], acc[:], RELU)
-                nc.scalar.dma_start(out[:, :HALF], early[:])
-            else:
-                nc.vector.tensor_scalar_max(ending[:, a - HALF : b - HALF], acc[:], 0.0)
-        nc.sync.dma_start(out[:, HALF:], ending[:])
+            if a < last:
+                nc.scalar.activation(early[:, a:b], acc[:], RELU)
+        nc.scalar.dma_start(out[:, :last], early[:])
+        nc.vector.tensor_scalar_max(ending[:], acc[:], 0.0)
+        nc.sync.dma_start(out[:, last:], ending[:])

@@ -13,6 +13,7 @@ U32 = mybir.dt.uint32
 U16 = mybir.dt.uint16
 U8 = mybir.dt.uint8
 FP8X4 = mybir.dt.float8_e4m3fn_x4
+MAX = mybir.AluOpType.max
 ADD = mybir.AluOpType.add
 MULT = mybir.AluOpType.mult
 SUBTRACT = mybir.AluOpType.subtract
@@ -178,49 +179,59 @@ def tile_picked_sagecat_maxrelu_p_kernel(tc, x_words, x_scales, w1, w2, w3, offs
         def columns(u):
             return slice(u * P, (u + 1) * P)
 
-        top = [psum.tile([P, PACK, P], F32, name="top%d" % u, tag="bank%d" % (PACK + u)) for u in range(V // P)]
-        nbr = [[plane_tile("nbr%d_" % d, t) for d in range(3)] for t in range(PACK)]
-        for t in range(PACK - 1):
-            for d in range(3):
-                fetch(nbr[t][d][:], pos_sb[d], t, 0, V)
-        for a, d in ((a, d) for a in (0, HALF) for d in range(3)):
-            fetch(nbr[PACK - 1][d][:, a : a + HALF], pos_sb[d], PACK - 1, a, a + HALF)
-        steps = [(t, 0, V) for t in range(PACK - 1)] + [(PACK - 1, 0, HALF), (PACK - 1, HALF, V)]
-        for n, (t, a, b) in enumerate(steps):
-            x, y, z = (nbr[t][d][:, a:b] for d in range(3))
-            tiles = range((b - a) // P)
-            lead, rest, third, extra = (
-                keep.tile([P, b - a], F32, name="%s%d" % (name, n), align_bytes=64) for name in ("lead", "rest", "third", "extra")
-            )
-            gain = keep.tile([P, b - a], F32, name="gain", tag="rest%d" % (n - 1), align_bytes=64)
-            nc.gpsimd.tensor_tensor(lead[:], y, x, SUBTRACT)
+        TURNED = PACK - 1
+        top = [psum.tile([P, TURNED, P], F32, name="top%d" % u, tag="bank%d" % (PACK + u)) for u in range(V // P)]
+        tiles = range(V // P)
+        for t in range(TURNED):
+            x, y, z = (plane_tile("nbr%d_" % d, t) for d in range(3))
+            for d, dst in enumerate((x, y, z)):
+                fetch(dst[:], pos_sb[d], t, 0, V)
+            lead, rest, third, extra = (plane_tile(name, t) for name in ("lead", "rest", "third", "extra"))
+            gain = keep.tile([P, V], F32, name="gain", tag="rest%d" % (t - 1), align_bytes=64)
+            nc.gpsimd.tensor_tensor(lead[:], y[:], x[:], SUBTRACT)
             nc.scalar.activation(gain[:], lead[:], RELU)
-            turned = psum.tile([P, b - a], F32, name="turned", tag="bank%d" % (min(n, PACK - 1) % 2))
+            turned = psum.tile([P, V], F32, name="turned", tag="bank%d" % (t % 2))
             for u in tiles:
                 turn(turned[:, columns(u)], z[:, columns(u)], True, True)
             nc.scalar.copy(third[:], turned[:])
-            nc.gpsimd.tensor_tensor(rest[:], x, z, SUBTRACT)
-            margin = psum.tile([P, b - a], F32, name="margin", tag="bank%d" % ((n + 1) % 2 if n < PACK else 2))
+            nc.gpsimd.tensor_tensor(rest[:], x[:], z[:], SUBTRACT)
+            margin = psum.tile([P, V], F32, name="margin", tag="bank%d" % ((t + 1) % 2))
             for term in (gain, rest):
                 for u in tiles:
                     turn(margin[:, columns(u)], term[:, columns(u)], term is gain and u == 0, term is rest and u == tiles[-1])
             nc.scalar.activation(extra[:], margin[:], RELU)
             for term, opens in ((third, True), (extra, False)):
                 for u in tiles:
-                    turn(top[a // P + u][:, t, :], term[:, columns(u)], opens, not opens)
+                    turn(top[u][:, t, :], term[:, columns(u)], opens, not opens)
 
+        x, y, z, pair, top3 = (keep.tile([P, V], BF16, name=name, align_bytes=64) for name in ("x3", "y3", "z3", "pair", "top3"))
+        lead = plane_tile("lead", TURNED)
+        gain = keep.tile([P, V], F32, name="gain", tag="rest%d" % (TURNED - 2), align_bytes=64)
+        halves = [slice(a, a + HALF) for a in (0, HALF)]
+        for half in halves:
+            for d, dst in enumerate((x, y)):
+                fetch(dst[:, half], pos_sb[d], TURNED, half.start, half.stop)
+            nc.gpsimd.tensor_tensor(lead[:, half], y[:, half], x[:, half], SUBTRACT)
+            nc.scalar.activation(gain[:, half], lead[:, half], RELU)
+        fetch(z[:], pos_sb[2], TURNED, 0, V)
+        for half in halves:
+            nc.gpsimd.tensor_tensor(pair[:, half], gain[:, half], x[:, half], ADD)
         top_bf = keep.tile([P, V, PACK], BF16, name="top_bf", align_bytes=64)
-        for u in range(V // P):
-            nc.scalar.copy(top_bf[:, columns(u), :], top[u][:].rearrange("p t v -> p v t"))
+        for u in tiles:
+            weave(top_bf[:, columns(u), :TURNED], top[u][:])
 
-        own = []
-        for u in range(2):
-            own.append(keep.tile([P, PACK, HALF], BF16, name="own%d" % u, tag="nbr%d_%d" % (1 - u, PACK - 2), align_bytes=64))
-            for t in range(PACK):
-                fetch(own[u][:, t, :], cen_sb, t, u * HALF, (u + 1) * HALF)
-        own_bf = [keep.tile([P, HALF, PACK], BF16, name="own_bf0", align_bytes=64)]
+        own = [keep.tile([P, PACK, HALF], BF16, name="own0", tag="nbr1_%d" % (TURNED - 1), align_bytes=64)]
+        for t in range(PACK):
+            fetch(own[0][:, t, :], cen_sb, t, 0, HALF)
+        nc.vector.tensor_tensor(top3[:], pair[:], z[:], MAX)
+        for half in halves:
+            nc.scalar.copy(top_bf[:, half, TURNED], top3[:, half])
+        own.append(keep.tile([P, PACK, HALF], BF16, name="own1", tag="z3", align_bytes=64))
+        for t in range(PACK):
+            fetch(own[1][:, t, :], cen_sb, t, HALF, V)
+        own_bf = [keep.tile([P, HALF, PACK], BF16, name="own_bf0", tag="pair", align_bytes=64)]
         nc.gpsimd.tensor_scalar(own_bf[0][:], own[0][:].rearrange("p t v -> p v t"), 1.0, 0.0, MULT, ADD)
-        own_bf.append(keep.tile([P, HALF, PACK], BF16, name="own_bf1", tag="extra%d" % PACK, align_bytes=64))
+        own_bf.append(keep.tile([P, HALF, PACK], BF16, name="own_bf1", align_bytes=64))
         for u in range(2):
             weave(own_bf[1][:, columns(u), :], own[1][:, :, columns(u)])
 
@@ -239,20 +250,21 @@ def tile_picked_sagecat_maxrelu_p_kernel(tc, x_words, x_scales, w1, w2, w3, offs
         last = CHUNKS[-1][0]
         early = keep.tile([P, last], F32, name="early", align_bytes=64)
         ending = keep.tile([P, V - last], F32, name="ending", align_bytes=64)
-        for n, (a, b) in enumerate(CHUNKS):
-            acc = psum.tile([P, b - a], F32, name="sum%d" % a, tag="bank%d" % n)
-            for e, (codes, scale) in ((1, (top_codes, top_scale)), (0, (own_codes, own_scale))):
-                nc.tensor.matmul_mx(
-                    out=acc[:],
-                    lhsT=w23_codes[:, e * N : (e + 1) * N].bitcast(FP8X4),
-                    lhsT_scale=w23_scale[:, e * N : (e + 1) * N],
-                    rhs=codes[:, a:b].bitcast(FP8X4),
-                    rhs_scale=scale[:, a:b],
-                    start=e == 1,
-                    stop=e == 0,
-                )
-            if a < last:
-                nc.scalar.activation(early[:, a:b], acc[:], RELU)
+        sums = [psum.tile([P, b - a], F32, name="sum%d" % a, tag="bank%d" % n) for n, (a, b) in enumerate(CHUNKS)]
+        operands = ((own_codes, own_scale), (top_codes, top_scale))
+        for n, e, opens in ((0, 0, True), (0, 1, False), (1, 1, True), (2, 1, True), (1, 0, False), (2, 0, False)):
+            a, b = CHUNKS[n]
+            nc.tensor.matmul_mx(
+                out=sums[n][:],
+                lhsT=w23_codes[:, e * N : (e + 1) * N].bitcast(FP8X4),
+                lhsT_scale=w23_scale[:, e * N : (e + 1) * N],
+                rhs=operands[e][0][:, a:b].bitcast(FP8X4),
+                rhs_scale=operands[e][1][:, a:b],
+                start=opens,
+                stop=not opens,
+            )
+        for acc, (a, b) in zip(sums[:-1], CHUNKS):
+            nc.scalar.activation(early[:, a:b], acc[:], RELU)
         nc.scalar.dma_start(out[:, :last], early[:])
-        nc.vector.tensor_scalar_max(ending[:], acc[:], 0.0)
+        nc.vector.tensor_scalar_max(ending[:], sums[-1][:], 0.0)
         nc.sync.dma_start(out[:, last:], ending[:])

@@ -180,8 +180,14 @@ def tile_picked_sagecat_maxrelu_p_kernel(tc, x_words, x_scales, w1, w2, w3, offs
             return slice(u * P, (u + 1) * P)
 
         TURNED = PACK - 1
-        top = [psum.tile([P, TURNED, P], F32, name="top%d" % u, tag="bank%d" % (PACK + u)) for u in range(V // P)]
+        top = keep.tile([P, PACK, V], BF16, name="top", align_bytes=64)
         tiles = range(V // P)
+
+        def turn_sum(bank, first, second):
+            for term in (first, second):
+                for u in tiles:
+                    turn(bank[:, columns(u)], term[:, columns(u)], term is first and u == 0, term is second and u == tiles[-1])
+
         for t in range(TURNED):
             x, y, z = (plane_tile("nbr%d_" % d, t) for d in range(3))
             for d, dst in enumerate((x, y, z)):
@@ -196,15 +202,13 @@ def tile_picked_sagecat_maxrelu_p_kernel(tc, x_words, x_scales, w1, w2, w3, offs
             nc.scalar.copy(third[:], turned[:])
             nc.gpsimd.tensor_tensor(rest[:], x[:], z[:], SUBTRACT)
             margin = psum.tile([P, V], F32, name="margin", tag="bank%d" % ((t + 1) % 2))
-            for term in (gain, rest):
-                for u in tiles:
-                    turn(margin[:, columns(u)], term[:, columns(u)], term is gain and u == 0, term is rest and u == tiles[-1])
+            turn_sum(margin, gain, rest)
             nc.scalar.activation(extra[:], margin[:], RELU)
-            for term, opens in ((third, True), (extra, False)):
-                for u in tiles:
-                    turn(top[u][:, t, :], term[:, columns(u)], opens, not opens)
+            back = psum.tile([P, V], F32, name="back", tag="bank%d" % (PACK + t))
+            turn_sum(back, third, extra)
+            nc.scalar.copy(top[:, t, :], back[:])
 
-        x, y, z, pair, top3 = (keep.tile([P, V], BF16, name=name, align_bytes=64) for name in ("x3", "y3", "z3", "pair", "top3"))
+        x, y, z, pair = (keep.tile([P, V], BF16, name=name, align_bytes=64) for name in ("x3", "y3", "z3", "pair"))
         lead = plane_tile("lead", TURNED)
         gain = keep.tile([P, V], F32, name="gain", tag="rest%d" % (TURNED - 2), align_bytes=64)
         halves = [slice(a, a + HALF) for a in (0, HALF)]
@@ -217,21 +221,19 @@ def tile_picked_sagecat_maxrelu_p_kernel(tc, x_words, x_scales, w1, w2, w3, offs
         for half in halves:
             nc.gpsimd.tensor_tensor(pair[:, half], gain[:, half], x[:, half], ADD)
         top_bf = keep.tile([P, V, PACK], BF16, name="top_bf", align_bytes=64)
-        for u in tiles:
-            weave(top_bf[:, columns(u), :TURNED], top[u][:])
 
         own = [keep.tile([P, PACK, HALF], BF16, name="own0", tag="nbr1_%d" % (TURNED - 1), align_bytes=64)]
         for t in range(PACK):
             fetch(own[0][:, t, :], cen_sb, t, 0, HALF)
-        nc.vector.tensor_tensor(top3[:], pair[:], z[:], MAX)
+        nc.vector.tensor_tensor(top[:, TURNED, :], pair[:], z[:], MAX)
         for half in halves:
-            nc.scalar.copy(top_bf[:, half, TURNED], top3[:, half])
+            weave(top_bf[:, half, :], top[:, :, half])
         own.append(keep.tile([P, PACK, HALF], BF16, name="own1", tag="z3", align_bytes=64))
         for t in range(PACK):
             fetch(own[1][:, t, :], cen_sb, t, HALF, V)
         own_bf = [keep.tile([P, HALF, PACK], BF16, name="own_bf0", tag="pair", align_bytes=64)]
         nc.gpsimd.tensor_scalar(own_bf[0][:], own[0][:].rearrange("p t v -> p v t"), 1.0, 0.0, MULT, ADD)
-        own_bf.append(keep.tile([P, HALF, PACK], BF16, name="own_bf1", align_bytes=64))
+        own_bf.append(keep.tile([P, HALF, PACK], BF16, name="own_bf1", tag="top", align_bytes=64))
         for u in range(2):
             weave(own_bf[1][:, columns(u), :], own[1][:, :, columns(u)])
 
@@ -248,7 +250,7 @@ def tile_picked_sagecat_maxrelu_p_kernel(tc, x_words, x_scales, w1, w2, w3, offs
             quantise(own_codes[:, a:b], own_scale[:, a:b], own_bf[1][:, a - HALF : b - HALF, :])
 
         last = CHUNKS[-1][0]
-        early = keep.tile([P, last], F32, name="early", align_bytes=64)
+        early = keep.tile([P, last], F32, name="early", tag="z3", align_bytes=64)
         ending = keep.tile([P, V - last], F32, name="ending", align_bytes=64)
         sums = [psum.tile([P, b - a], F32, name="sum%d" % a, tag="bank%d" % n) for n, (a, b) in enumerate(CHUNKS)]
         operands = ((own_codes, own_scale), (top_codes, top_scale))

@@ -48,8 +48,6 @@ def tile_picked_sagecat_maxrelu_p_kernel(tc, x_words, x_scales, w1, w2, w3, offs
         nc.vector.memset(table_scales[:, : T // 2].bitcast(I32), 0)
         nc.gpsimd.memset(table_scales[:, T // 2 :].bitcast(I32), 0)
         nc.vector.memset(x_scale[:].bitcast(I32), 0)
-        identity = keep.tile([P, P], F32, name="identity", align_bytes=64)
-        make_identity(nc, identity[:])
         words_hbm = x_words[0].rearrange("p c r -> p (c r)").bitcast(I32)
         w1_rows = w1.rearrange("(p j) c -> p j c", j=PACK)
         nc.sync.dma_start(table_words[:, :HEAD_COLS], words_hbm[:, :HEAD_COLS])
@@ -69,6 +67,8 @@ def tile_picked_sagecat_maxrelu_p_kernel(tc, x_words, x_scales, w1, w2, w3, offs
                 x_scale[first : first + QUADRANT // BLOCK_ROWS, :].bitcast(I32),
                 picked_scale[first : first + QUADRANT : BLOCK_ROWS, :].bitcast(I32),
             )
+        identity = keep.tile([P, P], F32, name="identity", tag="table_scales", align_bytes=64)
+        make_identity(nc, identity[:])
         x_codes = [keep.tile([P, BANK], U32, name="x_codes%d" % u, align_bytes=64) for u in range(S // BANK)]
         for u in range(S // BANK):
             entries = offs_sb[:, u * BANK // PER_COLUMN : (u + 1) * BANK // PER_COLUMN]
@@ -252,7 +252,7 @@ def tile_picked_sagecat_maxrelu_p_kernel(tc, x_words, x_scales, w1, w2, w3, offs
         last = CHUNKS[-1][0]
         early = keep.tile([P, last], F32, name="early", tag="z3", align_bytes=64)
         ending = keep.tile([P, V - last], F32, name="ending", align_bytes=64)
-        sums = [psum.tile([P, b - a], F32, name="sum%d" % a, tag="bank%d" % n) for n, (a, b) in enumerate(CHUNKS)]
+        sums = [psum.tile([P, b - a], F32, name="sum%d" % a, tag="bank%d" % (PACK + TURNED - 1 - n)) for n, (a, b) in enumerate(CHUNKS)]
         operands = ((own_codes, own_scale), (top_codes, top_scale))
         for n, e, opens in ((0, 0, True), (0, 1, False), (1, 1, True), (2, 1, True), (1, 0, False), (2, 0, False)):
             a, b = CHUNKS[n]

@@ -189,7 +189,8 @@ def tile_picked_sagecat_maxrelu_p_kernel(tc, x_words, x_scales, w1, w2, w3, offs
                     turn(bank[:, columns(u)], term[:, columns(u)], term is first and u == 0, term is second and u == tiles[-1])
 
         for t in range(TURNED):
-            x, y, z = (plane_tile("nbr%d_" % d, t) for d in range(3))
+            x, y = (keep.tile([P, V], BF16, name="nbr%d_%d" % (d, t), align_bytes=64) for d in range(2))
+            z = plane_tile("nbr2_", t)
             for d, dst in enumerate((x, y, z)):
                 fetch(dst[:], pos_sb[d], t, 0, V)
             lead, rest, third, extra = (plane_tile(name, t) for name in ("lead", "rest", "third", "extra"))
@@ -226,6 +227,8 @@ def tile_picked_sagecat_maxrelu_p_kernel(tc, x_words, x_scales, w1, w2, w3, offs
         for t in range(PACK):
             fetch(own[0][:, t, :], cen_sb, t, 0, HALF)
         nc.vector.tensor_tensor(top[:, TURNED, :], pair[:], z[:], MAX)
+        w23_codes = keep.tile([P, 2 * N], U32, name="w23_codes", tag="x3", align_bytes=64)
+        quantise(w23_codes[:], w23_scale[:], w23_bf[:])
         for half in halves:
             weave(top_bf[:, half, :], top[:, :, half])
         own.append(keep.tile([P, PACK, HALF], BF16, name="own1", tag="z3", align_bytes=64))
@@ -237,8 +240,6 @@ def tile_picked_sagecat_maxrelu_p_kernel(tc, x_words, x_scales, w1, w2, w3, offs
         for u in range(2):
             weave(own_bf[1][:, columns(u), :], own[1][:, :, columns(u)])
 
-        w23_codes = keep.tile([P, 2 * N], U32, name="w23_codes", tag="nbr1_%d" % (PACK - 2), align_bytes=64)
-        quantise(w23_codes[:], w23_scale[:], w23_bf[:])
         own_codes = keep.tile([P, V], U32, name="own_codes", align_bytes=64)
         own_scale = keep.tile([P, V], U8, name="own_scale", align_bytes=64)
         top_codes = keep.tile([P, V], U32, name="top_codes", align_bytes=64)

@@ -1,7 +1,6 @@
 from contextlib import ExitStack
 
 import concourse.mybir as mybir
-from concourse.masks import make_identity
 
 K, T, S, V, H, N = 512, 4096, 1024, 512, 512, 128
 FLOPS = 2 * K * H * S + 2 * 2 * H * N * V
@@ -16,8 +15,8 @@ FP8X4 = mybir.dt.float8_e4m3fn_x4
 MAX = mybir.AluOpType.max
 ADD = mybir.AluOpType.add
 MULT = mybir.AluOpType.mult
-SUBTRACT = mybir.AluOpType.subtract
 RELU = mybir.ActivationFunctionType.Relu
+COPY = mybir.ActivationFunctionType.Copy
 
 P = 128
 PACK = 4
@@ -37,13 +36,16 @@ def tile_picked_sagecat_maxrelu_p_kernel(tc, x_words, x_scales, w1, w2, w3, offs
         keep = ctx.enter_context(tc.tile_pool(name="keep", bufs=1))
         psum = ctx.enter_context(tc.psum_pool(name="psum", bufs=1))
 
+        def tile(shape, dtype, name, tag=None):
+            return keep.tile(shape, dtype, name=name, tag=tag or name, align_bytes=64)
+
         offs_sb = keep.tile([P, S // PER_COLUMN], U16, name="offs_sb")
         cen_sb = keep.tile([P, V // PER_COLUMN], U16, name="cen_sb")
         pos_sb = [keep.tile([P, V // PER_COLUMN], U16, name="pos_sb%d" % d) for d in range(3)]
-        table_words = keep.tile([P, T], I32, name="table_words", tag="table", align_bytes=64)
-        table_scales = keep.tile([P, T], U8, name="table_scales", align_bytes=64)
-        x_scale = keep.tile([P, S], U8, name="x_scale", align_bytes=64)
-        w1_raw = keep.tile([P, PACK, H], F32, name="w1_raw", tag="raw", align_bytes=64)
+        table_words = tile([P, T], I32, "table_words")
+        table_scales = tile([P, T], U8, "table_scales")
+        x_scale = tile([P, S], U8, "x_scale")
+        w1_raw = tile([P, PACK, H], F32, "w1_raw", "raw")
 
         nc.vector.memset(table_scales[:, : T // 2].bitcast(I32), 0)
         nc.gpsimd.memset(table_scales[:, T // 2 :].bitcast(I32), 0)
@@ -57,34 +59,35 @@ def tile_picked_sagecat_maxrelu_p_kernel(tc, x_words, x_scales, w1, w2, w3, offs
         nc.sync.dma_start(table_words[:, HEAD_COLS:], words_hbm[:, HEAD_COLS:])
         for e in range(2):
             nc.sync.dma_start(w1_raw[:, 2 * e : 2 * e + 2, :], w1_rows[:, 2 * e : 2 * e + 2, :])
-        for tile, pos in zip(pos_sb, (pos1, pos2, pos3)):
-            nc.sync.dma_start(tile[:], pos)
+        for dst, pos in zip(pos_sb, (pos1, pos2, pos3)):
+            nc.sync.dma_start(dst[:], pos)
 
-        picked_scale = keep.tile([P, S], U8, name="picked_scale", align_bytes=64)
+        picked_scale = tile([P, S], U8, "picked_scale")
         nc.vector.tensor_copy(picked_scale[:], table_scales[:].indirect(offs_sb[:]))
         for first in range(0, P, QUADRANT):
             nc.sync.dma_start(
                 x_scale[first : first + QUADRANT // BLOCK_ROWS, :].bitcast(I32),
                 picked_scale[first : first + QUADRANT : BLOCK_ROWS, :].bitcast(I32),
             )
-        identity = keep.tile([P, P], F32, name="identity", tag="table_scales", align_bytes=64)
-        make_identity(nc, identity[:])
-        x_codes = [keep.tile([P, BANK], U32, name="x_codes%d" % u, align_bytes=64) for u in range(S // BANK)]
+        x_codes = [tile([P, BANK], U32, "x_codes%d" % u) for u in range(S // BANK)]
         for u in range(S // BANK):
             entries = offs_sb[:, u * BANK // PER_COLUMN : (u + 1) * BANK // PER_COLUMN]
             nc.vector.tensor_copy(x_codes[u][:], table_words[:].bitcast(U32).indirect(entries))
 
         groups = ((0, 1), (1, PACK))
-        w1_bf = [keep.tile([P, hi - lo, P, PACK], BF16, name="w1_bf%d" % lo, tag="w1_bf%d" % lo, align_bytes=64) for lo, hi in groups]
-        w1_codes = [keep.tile([P, hi - lo, P], U32, name="w1_codes%d" % lo, tag="w1_codes" if lo == 0 else "w1_bf0", align_bytes=64) for lo, hi in groups]
-        w1_scale = keep.tile([P, PACK, P], U8, name="w1_scale", align_bytes=64)
-        h = [keep.tile([P, S], F32, name="h%d" % t, align_bytes=64) for t in range(PACK)]
+        w1_bf = [tile([P, hi - lo, P, PACK], BF16, "w1_bf%d" % lo) for lo, hi in groups]
+        w1_codes = [tile([P, hi - lo, P], U32, "w1_codes%d" % lo, "w1_codes" if lo == 0 else "w1_bf0") for lo, hi in groups]
+        w1_scale = tile([P, PACK, P], U8, "w1_scale")
+        h = [tile([P, S], F32, "h%d" % t) for t in range(PACK)]
 
         def quantise(codes, scale, woven):
             nc.vector.quantize_mx(out=codes.bitcast(FP8X4), scales=scale, in_=woven.rearrange("p c j -> p (c j)"))
 
-        def weave(dst, src):
-            nc.scalar.copy(dst.rearrange("p (c i) j -> p c j i", i=4), src.rearrange("p j (c i) -> p c j i", i=4))
+        def weave(copy, dst, src):
+            copy(dst.rearrange("p (c i) j -> p c j i", i=4), src.rearrange("p j (c i) -> p c j i", i=4))
+
+        def weave_aside(dst, src):
+            nc.gpsimd.tensor_scalar(dst, src.rearrange("p j c -> p c j"), 1.0, 0.0, MULT, ADD)
 
         def round_w1(copy, g, lo, hi, j0, j1):
             first = groups[g][0]
@@ -112,37 +115,17 @@ def tile_picked_sagecat_maxrelu_p_kernel(tc, x_words, x_scales, w1, w2, w3, offs
 
         def first_product(t, a, b):
             acc = next_bank(b - a, "acc")
-            for lo in range(a, b, BANK // 2):
-                u, c = divmod(lo, BANK)
-                nc.tensor.matmul_mx(
-                    out=acc[:, lo - a : lo - a + BANK // 2],
-                    lhsT=w1_codes[min(t, 1)][:, max(t - 1, 0), :].bitcast(FP8X4),
-                    lhsT_scale=w1_scale[:, t, :],
-                    rhs=x_codes[u][:, c : c + BANK // 2].bitcast(FP8X4),
-                    rhs_scale=x_scale[:, lo : lo + BANK // 2],
-                    start=True,
-                    stop=True,
-                )
-            return acc
-
-        def empty(t):
-            for (a, b), acc in products[t]:
-                if t == 0 and b == S:
-                    nc.vector.tensor_scalar_max(h[t][:, a:b], acc[:], 0.0)
-                else:
-                    nc.scalar.activation(h[t][:, a:b], acc[:], RELU)
-
-        idle = psum.tile([P, BANK], F32, name="idle", tag="bank%d" % (BANKS - 1))
-        for u in range(2):
+            u, c = divmod(a, BANK)
             nc.tensor.matmul_mx(
-                out=idle[:],
-                lhsT=x_codes[0][:, :P].bitcast(FP8X4),
-                lhsT_scale=picked_scale[:, :P],
-                rhs=x_codes[0][:].bitcast(FP8X4),
-                rhs_scale=picked_scale[:, :BANK],
+                out=acc[:],
+                lhsT=w1_codes[min(t, 1)][:, max(t - 1, 0), :].bitcast(FP8X4),
+                lhsT_scale=w1_scale[:, t, :],
+                rhs=x_codes[u][:, c : c + b - a].bitcast(FP8X4),
+                rhs_scale=x_scale[:, a:b],
                 start=True,
                 stop=True,
             )
+            return acc
 
         round_w1(nc.scalar.copy, 0, 0, 1, 0, 2)
         round_w1(nc.vector.tensor_copy, 0, 0, 1, 2, PACK)
@@ -153,119 +136,94 @@ def tile_picked_sagecat_maxrelu_p_kernel(tc, x_words, x_scales, w1, w2, w3, offs
         quantise_w1(0, 0, 1)
         quantise_w1(1, 1, 2)
         quantise_w1(1, 2, PACK)
-        products = []
         for t in range(PACK):
             width = BANK // 2 if t == 0 else BANK
-            products.append([((a, a + width), first_product(t, a, a + width)) for a in range(0, S, width)])
-            empty(t)
+            for a in range(0, S, width):
+                acc = first_product(t, a, a + width)
+                if t == 0 and a + width == S:
+                    nc.vector.tensor_scalar_max(h[t][:, a : a + width], acc[:], 0.0)
+                else:
+                    nc.scalar.activation(h[t][:, a : a + width], acc[:], RELU)
 
-        w23_bf = keep.tile([P, 2 * N, PACK], BF16, name="w23_bf", align_bytes=64)
-        w23_scale = keep.tile([P, 2 * N], U8, name="w23_scale", align_bytes=64)
-        w23_raw = keep.tile([P, PACK, 2 * N], F32, name="w23_raw", tag="raw", align_bytes=64)
+        w23_bf = tile([P, 2 * N, PACK], BF16, "w23_bf")
+        w23_scale = tile([P, 2 * N], U8, "w23_scale")
+        w23_codes = tile([P, 2 * N], U32, "w23_codes")
+        w23_raw = tile([P, PACK, 2 * N], F32, "w23_raw", "raw")
         for e, w in enumerate((w2, w3)):
             for t in range(PACK):
                 nc.sync.dma_start(w23_raw[:, t, e * N : (e + 1) * N], w.rearrange("(b t r) c -> t b r c", t=PACK, r=BLOCK_ROWS)[t])
-        weave(w23_bf[:], w23_raw[:])
+        weave_aside(w23_bf[:], w23_raw[:])
 
-        def fetch(dst, idx, t, a, b):
-            nc.vector.tensor_copy(dst, h[t][:].indirect(idx[:, a // PER_COLUMN : b // PER_COLUMN]))
+        def fetch_v(dst, idx, t, a=0, b=V):
+            nc.vector.tensor_copy(dst[:, a:b], h[t][:].indirect(idx[:, a // PER_COLUMN : b // PER_COLUMN]))
 
-        def plane_tile(name, t):
-            return keep.tile([P, V], F32, name="%s%d" % (name, t), align_bytes=64)
+        def fetch_s(dst, idx, t, a=0, b=V):
+            nc.scalar.activation(dst[:, a:b], h[t][:].indirect(idx[:, a // PER_COLUMN : b // PER_COLUMN]), COPY)
 
-        def turn(dst, term, start, stop):
-            nc.tensor.matmul(dst, term, identity[:], start=start, stop=stop, is_transpose=True)
+        def largest(dst, x, y, a=0, b=V):
+            nc.vector.tensor_tensor(dst[:, a:b], x[:, a:b], y[:, a:b], MAX)
 
-        def columns(u):
-            return slice(u * P, (u + 1) * P)
+        own = tile([P, PACK, V], BF16, "own")
+        own_bf = tile([P, V, PACK], BF16, "own_bf")
+        nbr = [[tile([P, V], BF16, "nbr%d_%d" % (t, d)) for d in range(3)] for t in range(PACK)]
+        top = tile([P, PACK, V], BF16, "top")
+        top_bf = tile([P, V, PACK], BF16, "top_bf")
+        own_codes = tile([P, V], U32, "own_codes")
+        own_scale = tile([P, V], U8, "own_scale")
+        top_codes = tile([P, V], U32, "top_codes")
+        top_scale = tile([P, V], U8, "top_scale")
 
-        TURNED = PACK - 1
-        top = keep.tile([P, PACK, V], BF16, name="top", align_bytes=64)
-        tiles = range(V // P)
-
-        def turn_sum(bank, first, second):
-            for term in (first, second):
-                for u in tiles:
-                    turn(bank[:, columns(u)], term[:, columns(u)], term is first and u == 0, term is second and u == tiles[-1])
-
-        for t in range(TURNED):
-            x, y = (keep.tile([P, V], BF16, name="nbr%d_%d" % (d, t), align_bytes=64) for d in range(2))
-            z = plane_tile("nbr2_", t)
-            for d, dst in enumerate((x, y, z)):
-                fetch(dst[:], pos_sb[d], t, 0, V)
-            lead, rest, third, extra = (plane_tile(name, t) for name in ("lead", "rest", "third", "extra"))
-            gain = keep.tile([P, V], F32, name="gain", tag="rest%d" % (t - 1), align_bytes=64)
-            nc.gpsimd.tensor_tensor(lead[:], y[:], x[:], SUBTRACT)
-            nc.scalar.activation(gain[:], lead[:], RELU)
-            turned = psum.tile([P, V], F32, name="turned", tag="bank%d" % (t % 2))
-            for u in tiles:
-                turn(turned[:, columns(u)], z[:, columns(u)], True, True)
-            nc.scalar.copy(third[:], turned[:])
-            nc.gpsimd.tensor_tensor(rest[:], x[:], z[:], SUBTRACT)
-            margin = psum.tile([P, V], F32, name="margin", tag="bank%d" % ((t + 1) % 2))
-            turn_sum(margin, gain, rest)
-            nc.scalar.activation(extra[:], margin[:], RELU)
-            back = psum.tile([P, V], F32, name="back", tag="bank%d" % (PACK + t))
-            turn_sum(back, third, extra)
-            nc.scalar.copy(top[:, t, :], back[:])
-
-        x, y, z, pair = (keep.tile([P, V], BF16, name=name, align_bytes=64) for name in ("x3", "y3", "z3", "pair"))
-        lead = plane_tile("lead", TURNED)
-        gain = keep.tile([P, V], F32, name="gain", tag="rest%d" % (TURNED - 2), align_bytes=64)
-        halves = [slice(a, a + HALF) for a in (0, HALF)]
-        for half in halves:
-            for d, dst in enumerate((x, y)):
-                fetch(dst[:, half], pos_sb[d], TURNED, half.start, half.stop)
-            nc.gpsimd.tensor_tensor(lead[:, half], y[:, half], x[:, half], SUBTRACT)
-            nc.scalar.activation(gain[:, half], lead[:, half], RELU)
-        fetch(z[:], pos_sb[2], TURNED, 0, V)
-        for half in halves:
-            nc.gpsimd.tensor_tensor(pair[:, half], gain[:, half], x[:, half], ADD)
-        top_bf = keep.tile([P, V, PACK], BF16, name="top_bf", align_bytes=64)
-
-        own = [keep.tile([P, PACK, HALF], BF16, name="own0", tag="nbr1_%d" % (TURNED - 1), align_bytes=64)]
-        for t in range(PACK):
-            fetch(own[0][:, t, :], cen_sb, t, 0, HALF)
-        nc.vector.tensor_tensor(top[:, TURNED, :], pair[:], z[:], MAX)
-        w23_codes = keep.tile([P, 2 * N], U32, name="w23_codes", tag="x3", align_bytes=64)
+        fetch_v(own[:, 0, :], cen_sb, 0)
+        for t in range(1, PACK):
+            fetch_s(own[:, t, :], cen_sb, t)
+        for d in range(3):
+            fetch_v(nbr[0][d], pos_sb[d], 0)
+        pair0 = tile([P, V], BF16, "pair0")
+        largest(pair0, nbr[0][0], nbr[0][1])
+        fetch_v(nbr[1][0], pos_sb[0], 1)
+        largest(top[:, 0, :], pair0, nbr[0][2])
         quantise(w23_codes[:], w23_scale[:], w23_bf[:])
-        for half in halves:
-            weave(top_bf[:, half, :], top[:, :, half])
-        own.append(keep.tile([P, PACK, HALF], BF16, name="own1", tag="z3", align_bytes=64))
-        for t in range(PACK):
-            fetch(own[1][:, t, :], cen_sb, t, HALF, V)
-        own_bf = [keep.tile([P, HALF, PACK], BF16, name="own_bf0", tag="pair", align_bytes=64)]
-        nc.gpsimd.tensor_scalar(own_bf[0][:], own[0][:].rearrange("p t v -> p v t"), 1.0, 0.0, MULT, ADD)
-        own_bf.append(keep.tile([P, HALF, PACK], BF16, name="own_bf1", tag="top", align_bytes=64))
-        for u in range(2):
-            weave(own_bf[1][:, columns(u), :], own[1][:, :, columns(u)])
-
-        own_codes = keep.tile([P, V], U32, name="own_codes", align_bytes=64)
-        own_scale = keep.tile([P, V], U8, name="own_scale", align_bytes=64)
-        top_codes = keep.tile([P, V], U32, name="top_codes", align_bytes=64)
-        top_scale = keep.tile([P, V], U8, name="top_scale", align_bytes=64)
-        quantise(own_codes[:, :HALF], own_scale[:, :HALF], own_bf[0][:])
-        for a in range(0, V, HALF):
-            quantise(top_codes[:, a : a + HALF], top_scale[:, a : a + HALF], top_bf[:, a : a + HALF, :])
-        for a, b in CHUNKS[1:]:
-            quantise(own_codes[:, a:b], own_scale[:, a:b], own_bf[1][:, a - HALF : b - HALF, :])
+        weave_aside(own_bf[:], own[:])
+        for d in range(1, 3):
+            fetch_v(nbr[1][d], pos_sb[d], 1)
+        fetch_v(nbr[3][0], pos_sb[0], 3)
+        for d in range(3):
+            fetch_s(nbr[2][d], pos_sb[d], 2)
+        fetch_s(nbr[3][1], pos_sb[1], 3)
+        fetch_s(nbr[3][2], pos_sb[2], 3, 0, HALF)
+        fetch_s(nbr[3][2], pos_sb[2], 3, HALF, V)
+        pair = tile([P, PACK - 1, V], BF16, "pair", "own")
+        largest(pair[:, 0, :], nbr[1][0], nbr[1][1])
+        quantise(own_codes[:], own_scale[:], own_bf[:])
+        largest(top[:, 1, :], pair[:, 0, :], nbr[1][2])
+        largest(pair[:, 1, :], nbr[2][0], nbr[2][1])
+        largest(pair[:, 2, :], nbr[3][0], nbr[3][1])
+        largest(top[:, 2, :], pair[:, 1, :], nbr[2][2])
+        largest(top[:, 3, :], pair[:, 2, :], nbr[3][2], 0, HALF)
+        (a0, b0), (a1, b1), (a2, b2) = CHUNKS
+        weave(nc.vector.tensor_copy, top_bf[:, a0:b0, :], top[:, :, a0:b0])
+        largest(top[:, 3, :], pair[:, 2, :], nbr[3][2], HALF, V)
+        quantise(top_codes[:, a0:b0], top_scale[:, a0:b0], top_bf[:, a0:b0, :])
+        weave(nc.scalar.copy, top_bf[:, a2:b2, :], top[:, :, a2:b2])
+        weave(nc.vector.tensor_copy, top_bf[:, a1:b1, :], top[:, :, a1:b1])
+        quantise(top_codes[:, a1:b1], top_scale[:, a1:b1], top_bf[:, a1:b1, :])
+        quantise(top_codes[:, a2:b2], top_scale[:, a2:b2], top_bf[:, a2:b2, :])
 
         last = CHUNKS[-1][0]
-        early = keep.tile([P, last], F32, name="early", tag="z3", align_bytes=64)
-        ending = keep.tile([P, V - last], F32, name="ending", align_bytes=64)
-        sums = [psum.tile([P, b - a], F32, name="sum%d" % a, tag="bank%d" % (PACK + TURNED - 1 - n)) for n, (a, b) in enumerate(CHUNKS)]
-        operands = ((own_codes, own_scale), (top_codes, top_scale))
-        for n, e, opens in ((0, 0, True), (0, 1, False), (1, 1, True), (2, 1, True), (1, 0, False), (2, 0, False)):
-            a, b = CHUNKS[n]
-            nc.tensor.matmul_mx(
-                out=sums[n][:],
-                lhsT=w23_codes[:, e * N : (e + 1) * N].bitcast(FP8X4),
-                lhsT_scale=w23_scale[:, e * N : (e + 1) * N],
-                rhs=operands[e][0][:, a:b].bitcast(FP8X4),
-                rhs_scale=operands[e][1][:, a:b],
-                start=opens,
-                stop=not opens,
-            )
+        early = tile([P, last], F32, "early")
+        ending = tile([P, V - last], F32, "ending")
+        sums = [next_bank(b - a, "sum") for a, b in CHUNKS]
+        for e, (codes, scale) in enumerate(((own_codes, own_scale), (top_codes, top_scale))):
+            for acc, (a, b) in zip(sums, CHUNKS):
+                nc.tensor.matmul_mx(
+                    out=acc[:],
+                    lhsT=w23_codes[:, e * N : (e + 1) * N].bitcast(FP8X4),
+                    lhsT_scale=w23_scale[:, e * N : (e + 1) * N],
+                    rhs=codes[:, a:b].bitcast(FP8X4),
+                    rhs_scale=scale[:, a:b],
+                    start=e == 0,
+                    stop=e == 1,
+                )
         for acc, (a, b) in zip(sums[:-1], CHUNKS):
             nc.scalar.activation(early[:, a:b], acc[:], RELU)
         nc.scalar.dma_start(out[:, :last], early[:])

@@ -27,6 +27,7 @@ BANK = 512
 BANKS = 8
 HEAD_COLS = 1024
 HALF = V // 2
+WARM_PASSES, WARM_COLUMNS = 3, 32
 CHUNKS = ((0, HALF), (HALF, HALF + P), (HALF + P, V))
 
 
@@ -126,6 +127,18 @@ def tile_picked_sagecat_maxrelu_p_kernel(tc, x_words, x_scales, w1, w2, w3, offs
                 stop=True,
             )
             return acc
+
+        idle = psum.tile([P, BANK], F32, name="idle", tag="bank%d" % (BANKS - 1))
+        for u in range(WARM_PASSES):
+            nc.tensor.matmul_mx(
+                out=idle[:WARM_COLUMNS, :],
+                lhsT=x_codes[0][:, :WARM_COLUMNS].bitcast(FP8X4),
+                lhsT_scale=picked_scale[:, :WARM_COLUMNS],
+                rhs=x_codes[0][:].bitcast(FP8X4),
+                rhs_scale=picked_scale[:, :BANK],
+                start=True,
+                stop=True,
+            )
 
         round_w1(nc.scalar.copy, 0, 0, 1, 0, 2)
         round_w1(nc.vector.tensor_copy, 0, 0, 1, 2, PACK)

@@ -217,7 +217,7 @@ def tile_picked_sagecat_maxrelu_p_kernel(tc, x_words, x_scales, w1, w2, w3, offs
         weave(nc.vector.tensor_copy, top_bf[:, a0:b0, :], top[:, :, a0:b0])
         largest(top[:, 3, :], pair[:, 2, :], nbr[3][2], HALF, V)
         quantise(top_codes[:, a0:b0], top_scale[:, a0:b0], top_bf[:, a0:b0, :])
-        weave(nc.scalar.copy, top_bf[:, a2:b2, :], top[:, :, a2:b2])
+        nc.scalar.copy(top_bf[:, a2:b2, :], top[:, :, a2:b2].rearrange("p j c -> p c j"))
         weave(nc.vector.tensor_copy, top_bf[:, a1:b1, :], top[:, :, a1:b1])
         quantise(top_codes[:, a1:b1], top_scale[:, a1:b1], top_bf[:, a1:b1, :])
         quantise(top_codes[:, a2:b2], top_scale[:, a2:b2], top_bf[:, a2:b2, :])

@@ -25,10 +25,10 @@ QUADRANT = 32
 PER_COLUMN = 16
 BANK = 512
 BANKS = 8
-HEAD_COLS = 1024
 HALF = V // 2
-WARM_PASSES, WARM_COLUMNS = 3, 32
 CHUNKS = ((0, HALF), (HALF, HALF + P), (HALF + P, V))
+HEAD_COLS = 1024
+WARM_PASSES, WARM_COLUMNS = 3, 32
 
 
 def tile_picked_sagecat_maxrelu_p_kernel(tc, x_words, x_scales, w1, w2, w3, offs, cen, pos1, pos2, pos3, out):
@@ -40,6 +40,19 @@ def tile_picked_sagecat_maxrelu_p_kernel(tc, x_words, x_scales, w1, w2, w3, offs
         def tile(shape, dtype, name, tag=None):
             return keep.tile(shape, dtype, name=name, tag=tag or name, align_bytes=64)
 
+        def quantise(codes, scale, woven):
+            nc.vector.quantize_mx(out=codes.bitcast(FP8X4), scales=scale, in_=woven.rearrange("p c j -> p (c j)"))
+
+        def weave_aside(dst, src):
+            nc.gpsimd.tensor_scalar(dst, src, 1.0, 0.0, MULT, ADD)
+
+        banks = []
+
+        def next_bank(width, name):
+            acc = psum.tile([P, width], F32, name=name, tag="bank%d" % (len(banks) % BANKS))
+            banks.append(acc)
+            return acc
+
         offs_sb = keep.tile([P, S // PER_COLUMN], U16, name="offs_sb")
         cen_sb = keep.tile([P, V // PER_COLUMN], U16, name="cen_sb")
         pos_sb = [keep.tile([P, V // PER_COLUMN], U16, name="pos_sb%d" % d) for d in range(3)]
@@ -47,12 +60,13 @@ def tile_picked_sagecat_maxrelu_p_kernel(tc, x_words, x_scales, w1, w2, w3, offs
         table_scales = tile([P, T], U8, "table_scales")
         x_scale = tile([P, S], U8, "x_scale")
         w1_raw = tile([P, PACK, H], F32, "w1_raw", "raw")
+        words_hbm = x_words[0].rearrange("p c r -> p (c r)").bitcast(I32)
+        w1_rows = w1.rearrange("(p j) c -> p j c", j=PACK)
+        h = [tile([P, S], F32, "h%d" % t) for t in range(PACK)]
 
         nc.vector.memset(table_scales[:, : T // 2].bitcast(I32), 0)
         nc.gpsimd.memset(table_scales[:, T // 2 :].bitcast(I32), 0)
         nc.vector.memset(x_scale[:].bitcast(I32), 0)
-        words_hbm = x_words[0].rearrange("p c r -> p (c r)").bitcast(I32)
-        w1_rows = w1.rearrange("(p j) c -> p j c", j=PACK)
         nc.sync.dma_start(table_words[:, :HEAD_COLS], words_hbm[:, :HEAD_COLS])
         nc.sync.dma_start(offs_sb[:], offs)
         nc.sync.dma_start(cen_sb[:], cen)
@@ -79,16 +93,6 @@ def tile_picked_sagecat_maxrelu_p_kernel(tc, x_words, x_scales, w1, w2, w3, offs
         w1_bf = [tile([P, hi - lo, P, PACK], BF16, "w1_bf%d" % lo) for lo, hi in groups]
         w1_codes = [tile([P, hi - lo, P], U32, "w1_codes%d" % lo, "w1_codes" if lo == 0 else "w1_bf0") for lo, hi in groups]
         w1_scale = tile([P, PACK, P], U8, "w1_scale")
-        h = [tile([P, S], F32, "h%d" % t) for t in range(PACK)]
-
-        def quantise(codes, scale, woven):
-            nc.vector.quantize_mx(out=codes.bitcast(FP8X4), scales=scale, in_=woven.rearrange("p c j -> p (c j)"))
-
-        def weave(copy, dst, src):
-            copy(dst.rearrange("p (c i) j -> p c j i", i=4), src.rearrange("p j (c i) -> p c j i", i=4))
-
-        def weave_aside(dst, src):
-            nc.gpsimd.tensor_scalar(dst, src.rearrange("p j c -> p c j"), 1.0, 0.0, MULT, ADD)
 
         def round_w1(copy, g, lo, hi, j0, j1):
             first = groups[g][0]
@@ -106,13 +110,6 @@ def tile_picked_sagecat_maxrelu_p_kernel(tc, x_words, x_scales, w1, w2, w3, offs
                 w1_scale[:, lo:hi, :].rearrange("p t m -> p (t m)"),
                 w1_bf[g][:, lo - first : hi - first].rearrange("p t m j -> p (t m) j"),
             )
-
-        banks = []
-
-        def next_bank(width, name):
-            acc = psum.tile([P, width], F32, name=name, tag="bank%d" % (len(banks) % BANKS))
-            banks.append(acc)
-            return acc
 
         def first_product(t, a, b):
             acc = next_bank(b - a, "acc")
@@ -165,62 +162,64 @@ def tile_picked_sagecat_maxrelu_p_kernel(tc, x_words, x_scales, w1, w2, w3, offs
         for e, w in enumerate((w2, w3)):
             for t in range(PACK):
                 nc.sync.dma_start(w23_raw[:, t, e * N : (e + 1) * N], w.rearrange("(b t r) c -> t b r c", t=PACK, r=BLOCK_ROWS)[t])
-        weave_aside(w23_bf[:], w23_raw[:])
+        weave_aside(w23_bf[:], w23_raw[:].rearrange("p j c -> p c j"))
 
         def fetch_v(dst, idx, t, a=0, b=V):
-            nc.vector.tensor_copy(dst[:, a:b], h[t][:].indirect(idx[:, a // PER_COLUMN : b // PER_COLUMN]))
+            nc.vector.tensor_copy(dst, h[t][:].indirect(idx[:, a // PER_COLUMN : b // PER_COLUMN]))
 
         def fetch_s(dst, idx, t, a=0, b=V):
-            nc.scalar.activation(dst[:, a:b], h[t][:].indirect(idx[:, a // PER_COLUMN : b // PER_COLUMN]), COPY)
-
-        def largest(dst, x, y, a=0, b=V):
-            nc.vector.tensor_tensor(dst[:, a:b], x[:, a:b], y[:, a:b], MAX)
+            nc.scalar.activation(dst, h[t][:].indirect(idx[:, a // PER_COLUMN : b // PER_COLUMN]), COPY)
 
         own = tile([P, PACK, V], BF16, "own")
         own_bf = tile([P, V, PACK], BF16, "own_bf")
-        nbr = [[tile([P, V], BF16, "nbr%d_%d" % (t, d)) for d in range(3)] for t in range(PACK)]
-        top = tile([P, PACK, V], BF16, "top")
+        nbr = [tile([P, 2, V, 2], BF16, "nbr%d" % d) for d in range(3)]
+        both = tile([P, 2, V, 2], BF16, "both")
         top_bf = tile([P, V, PACK], BF16, "top_bf")
         own_codes = tile([P, V], U32, "own_codes")
         own_scale = tile([P, V], U8, "own_scale")
         top_codes = tile([P, V], U32, "top_codes")
         top_scale = tile([P, V], U8, "top_scale")
 
-        fetch_v(own[:, 0, :], cen_sb, 0)
-        for t in range(1, PACK):
-            fetch_s(own[:, t, :], cen_sb, t)
-        for d in range(3):
-            fetch_v(nbr[0][d], pos_sb[d], 0)
-        pair0 = tile([P, V], BF16, "pair0")
-        largest(pair0, nbr[0][0], nbr[0][1])
-        fetch_v(nbr[1][0], pos_sb[0], 1)
-        largest(top[:, 0, :], pair0, nbr[0][2])
-        quantise(w23_codes[:], w23_scale[:], w23_bf[:])
-        weave_aside(own_bf[:], own[:])
-        for d in range(1, 3):
-            fetch_v(nbr[1][d], pos_sb[d], 1)
-        fetch_v(nbr[3][0], pos_sb[0], 3)
-        for d in range(3):
-            fetch_s(nbr[2][d], pos_sb[d], 2)
-        fetch_s(nbr[3][1], pos_sb[1], 3)
-        fetch_s(nbr[3][2], pos_sb[2], 3, 0, HALF)
-        fetch_s(nbr[3][2], pos_sb[2], 3, HALF, V)
-        pair = tile([P, PACK - 1, V], BF16, "pair", "own")
-        largest(pair[:, 0, :], nbr[1][0], nbr[1][1])
-        quantise(own_codes[:], own_scale[:], own_bf[:])
-        largest(top[:, 1, :], pair[:, 0, :], nbr[1][2])
-        largest(pair[:, 1, :], nbr[2][0], nbr[2][1])
-        largest(pair[:, 2, :], nbr[3][0], nbr[3][1])
-        largest(top[:, 2, :], pair[:, 1, :], nbr[2][2])
-        largest(top[:, 3, :], pair[:, 2, :], nbr[3][2], 0, HALF)
+        def fetch_pair(fetch, d, u, a=0, b=V):
+            for e in range(2):
+                fetch(nbr[d][:, u, a:b, e], pos_sb[d], 2 * u + e, a, b)
+
+        def finish(a, b):
+            nc.vector.tensor_tensor(
+                top_bf[:, a:b, :].rearrange("p v (u e) -> p v u e", e=2),
+                both[:, :, a:b, :].rearrange("p u v e -> p v u e"),
+                nbr[2][:, :, a:b, :].rearrange("p u v e -> p v u e"),
+                MAX,
+            )
+
+        def quantise_top(a, b):
+            quantise(top_codes[:, a:b], top_scale[:, a:b], top_bf[:, a:b, :])
+
         (a0, b0), (a1, b1), (a2, b2) = CHUNKS
-        weave(nc.vector.tensor_copy, top_bf[:, a0:b0, :], top[:, :, a0:b0])
-        largest(top[:, 3, :], pair[:, 2, :], nbr[3][2], HALF, V)
-        quantise(top_codes[:, a0:b0], top_scale[:, a0:b0], top_bf[:, a0:b0, :])
-        nc.scalar.copy(top_bf[:, a2:b2, :], top[:, :, a2:b2].rearrange("p j c -> p c j"))
-        weave(nc.vector.tensor_copy, top_bf[:, a1:b1, :], top[:, :, a1:b1])
-        quantise(top_codes[:, a1:b1], top_scale[:, a1:b1], top_bf[:, a1:b1, :])
-        quantise(top_codes[:, a2:b2], top_scale[:, a2:b2], top_bf[:, a2:b2, :])
+
+        fetch_v(own[:, 0, :], cen_sb, 0)
+        fetch_v(nbr[0][:, 0, :, 0], pos_sb[0], 0)
+        fetch_v(own[:, 1, :], cen_sb, 1)
+        fetch_v(nbr[0][:, 0, :, 1], pos_sb[0], 1)
+        for t in range(2, PACK):
+            fetch_s(own[:, t, :], cen_sb, t)
+        weave_aside(own_bf[:], own[:].rearrange("p j c -> p c j"))
+        fetch_pair(fetch_v, 1, 0)
+        fetch_pair(fetch_v, 2, 0)
+        fetch_pair(fetch_v, 2, 1, b1, V)
+        for d in range(2):
+            fetch_pair(fetch_s, d, 1)
+        fetch_pair(fetch_s, 2, 1, 0, HALF)
+        fetch_pair(fetch_s, 2, 1, HALF, b1)
+        quantise(w23_codes[:], w23_scale[:], w23_bf[:])
+        quantise(own_codes[:], own_scale[:], own_bf[:])
+        nc.vector.tensor_tensor(both[:], nbr[0][:], nbr[1][:], MAX)
+        finish(a0, b0)
+        finish(a2, b2)
+        quantise_top(a0, b0)
+        finish(a1, b1)
+        quantise_top(a2, b2)
+        quantise_top(a1, b1)
 
         last = CHUNKS[-1][0]
         early = tile([P, last], F32, "early")

@@ -150,7 +150,7 @@ def tile_picked_sagecat_maxrelu_p_kernel(tc, x_words, x_scales, w1, w2, w3, offs
             width = BANK // 2 if t == 0 else BANK
             for a in range(0, S, width):
                 acc = first_product(t, a, a + width)
-                if t == 0 and a + width == S:
+                if t == 0 and a % BANK == 0:
                     nc.vector.tensor_scalar_max(h[t][:, a : a + width], acc[:], 0.0)
                 else:
                     nc.scalar.activation(h[t][:, a : a + width], acc[:], RELU)
@@ -206,24 +206,22 @@ def tile_picked_sagecat_maxrelu_p_kernel(tc, x_words, x_scales, w1, w2, w3, offs
         weave_aside(own_bf[:], own[:].rearrange("p j c -> p c j"))
         fetch_pair(fetch_v, 1, 0)
         fetch_pair(fetch_v, 2, 0)
-        fetch_pair(fetch_v, 2, 1, b1, V)
+        fetch_pair(fetch_v, 2, 1, a1, b1)
         for d in range(2):
             fetch_pair(fetch_s, d, 1)
-        fetch_pair(fetch_s, 2, 1, 0, HALF)
-        fetch_pair(fetch_s, 2, 1, HALF, b1)
+        fetch_pair(fetch_s, 2, 1, a0, b0)
+        fetch_pair(fetch_s, 2, 1, a2, b2)
         quantise(w23_codes[:], w23_scale[:], w23_bf[:])
-        quantise(own_codes[:], own_scale[:], own_bf[:])
         nc.vector.tensor_tensor(both[:], nbr[0][:], nbr[1][:], MAX)
+        quantise(own_codes[:], own_scale[:], own_bf[:])
         finish(a0, b0)
-        finish(a2, b2)
-        quantise_top(a0, b0)
         finish(a1, b1)
-        quantise_top(a2, b2)
+        quantise_top(a0, b0)
+        finish(a2, b2)
         quantise_top(a1, b1)
+        quantise_top(a2, b2)
 
-        last = CHUNKS[-1][0]
-        early = tile([P, last], F32, "early")
-        ending = tile([P, V - last], F32, "ending")
+        done = [tile([P, b - a], F32, "done%d" % a) for a, b in CHUNKS]
         sums = [next_bank(b - a, "sum") for a, b in CHUNKS]
         for e, (codes, scale) in enumerate(((own_codes, own_scale), (top_codes, top_scale))):
             for acc, (a, b) in zip(sums, CHUNKS):
@@ -236,8 +234,9 @@ def tile_picked_sagecat_maxrelu_p_kernel(tc, x_words, x_scales, w1, w2, w3, offs
                     start=e == 0,
                     stop=e == 1,
                 )
-        for acc, (a, b) in zip(sums[:-1], CHUNKS):
-            nc.scalar.activation(early[:, a:b], acc[:], RELU)
-        nc.scalar.dma_start(out[:, :last], early[:])
-        nc.vector.tensor_scalar_max(ending[:], sums[-1][:], 0.0)
-        nc.sync.dma_start(out[:, last:], ending[:])
+        nc.scalar.activation(done[0][:], sums[0][:], RELU)
+        nc.sync.dma_start(out[:, a0:b0], done[0][:])
+        nc.scalar.activation(done[1][:], sums[1][:], RELU)
+        nc.scalar.dma_start(out[:, a1:b1], done[1][:])
+        nc.vector.tensor_scalar_max(done[2][:], sums[2][:], 0.0)
+        nc.sync.dma_start(out[:, a2:b2], done[2][:])

@@ -221,7 +221,7 @@ def tile_picked_sagecat_maxrelu_p_kernel(tc, x_words, x_scales, w1, w2, w3, offs
         quantise_top(a1, b1)
         quantise_top(a2, b2)
 
-        done = [tile([P, b - a], F32, "done%d" % a) for a, b in CHUNKS]
+        done = tile([P, V], F32, "done")
         sums = [next_bank(b - a, "sum") for a, b in CHUNKS]
         for e, (codes, scale) in enumerate(((own_codes, own_scale), (top_codes, top_scale))):
             for acc, (a, b) in zip(sums, CHUNKS):
@@ -234,9 +234,7 @@ def tile_picked_sagecat_maxrelu_p_kernel(tc, x_words, x_scales, w1, w2, w3, offs
                     start=e == 0,
                     stop=e == 1,
                 )
-        nc.scalar.activation(done[0][:], sums[0][:], RELU)
-        nc.sync.dma_start(out[:, a0:b0], done[0][:])
-        nc.scalar.activation(done[1][:], sums[1][:], RELU)
-        nc.scalar.dma_start(out[:, a1:b1], done[1][:])
-        nc.vector.tensor_scalar_max(done[2][:], sums[2][:], 0.0)
-        nc.sync.dma_start(out[:, a2:b2], done[2][:])
+        for acc, (a, b) in zip(sums[:-1], CHUNKS):
+            nc.scalar.activation(done[:, a:b], acc[:], RELU)
+        nc.vector.tensor_scalar_max(done[:, a2:b2], sums[-1][:], 0.0)
+        nc.sync.dma_start(out, done[:])

@@ -206,13 +206,13 @@ def tile_picked_sagecat_maxrelu_p_kernel(tc, x_words, x_scales, w1, w2, w3, offs
         weave_aside(own_bf[:], own[:].rearrange("p j c -> p c j"))
         fetch_pair(fetch_v, 1, 0)
         fetch_pair(fetch_v, 2, 0)
-        fetch_pair(fetch_v, 2, 1, a1, b1)
         for d in range(2):
             fetch_pair(fetch_s, d, 1)
-        fetch_pair(fetch_s, 2, 1, a0, b0)
-        fetch_pair(fetch_s, 2, 1, a2, b2)
+        for a, b in CHUNKS:
+            fetch_pair(fetch_s, 2, 1, a, b)
         quantise(w23_codes[:], w23_scale[:], w23_bf[:])
-        nc.vector.tensor_tensor(both[:], nbr[0][:], nbr[1][:], MAX)
+        for u in range(2):
+            nc.vector.tensor_tensor(both[:, u], nbr[0][:, u], nbr[1][:, u], MAX)
         quantise(own_codes[:], own_scale[:], own_bf[:])
         finish(a0, b0)
         finish(a1, b1)
@@ -234,7 +234,6 @@ def tile_picked_sagecat_maxrelu_p_kernel(tc, x_words, x_scales, w1, w2, w3, offs
                     start=e == 0,
                     stop=e == 1,
                 )
-        for acc, (a, b) in zip(sums[:-1], CHUNKS):
+        for acc, (a, b) in zip(sums, CHUNKS):
             nc.scalar.activation(done[:, a:b], acc[:], RELU)
-        nc.vector.tensor_scalar_max(done[:, a2:b2], sums[-1][:], 0.0)
-        nc.sync.dma_start(out, done[:])
+        nc.scalar.dma_start(out, done[:])

@@ -234,6 +234,7 @@ def tile_picked_sagecat_maxrelu_p_kernel(tc, x_words, x_scales, w1, w2, w3, offs
                     start=e == 0,
                     stop=e == 1,
                 )
-        for acc, (a, b) in zip(sums, CHUNKS):
+        for acc, (a, b) in zip(sums[:-1], CHUNKS):
             nc.scalar.activation(done[:, a:b], acc[:], RELU)
-        nc.scalar.dma_start(out, done[:])
+        nc.vector.tensor_scalar_max(done[:, a2:b2], sums[-1][:], 0.0)
+        nc.sync.dma_start(out, done[:])

@@ -146,14 +146,15 @@ def tile_picked_sagecat_maxrelu_p_kernel(tc, x_words, x_scales, w1, w2, w3, offs
         quantise_w1(0, 0, 1)
         quantise_w1(1, 1, 2)
         quantise_w1(1, 2, PACK)
-        for t in range(PACK):
-            width = BANK // 2 if t == 0 else BANK
-            for a in range(0, S, width):
-                acc = first_product(t, a, a + width)
-                if t == 0 and a % BANK == 0:
-                    nc.vector.tensor_scalar_max(h[t][:, a : a + width], acc[:], 0.0)
-                else:
-                    nc.scalar.activation(h[t][:, a : a + width], acc[:], RELU)
+        narrow = BANK // 2
+        stretches = [(0, a, a + narrow) for a in range(0, S, narrow)] + [(1, 0, narrow), (1, narrow, BANK), (1, BANK, S)]
+        stretches = stretches + [(t, a, a + BANK) for t in range(2, PACK) for a in range(0, S, BANK)]
+        for t, a, b in stretches:
+            acc = first_product(t, a, b)
+            if b - a == narrow and a % BANK == 0:
+                nc.vector.tensor_scalar_max(h[t][:, a:b], acc[:], 0.0)
+            else:
+                nc.scalar.activation(h[t][:, a:b], acc[:], RELU)
 
         w23_bf = tile([P, 2 * N, PACK], BF16, "w23_bf")
         w23_scale = tile([P, 2 * N], U8, "w23_scale")
@@ -203,7 +204,8 @@ def tile_picked_sagecat_maxrelu_p_kernel(tc, x_words, x_scales, w1, w2, w3, offs
         fetch_v(nbr[0][:, 0, :, 1], pos_sb[0], 1)
         for t in range(2, PACK):
             fetch_s(own[:, t, :], cen_sb, t)
-        weave_aside(own_bf[:], own[:].rearrange("p j c -> p c j"))
+        for a in range(0, V, HALF):
+            weave_aside(own_bf[:, a : a + HALF, :], own[:, :, a : a + HALF].rearrange("p j c -> p c j"))
         fetch_pair(fetch_v, 1, 0)
         fetch_pair(fetch_v, 2, 0)
         for d in range(2):
@@ -213,8 +215,9 @@ def tile_picked_sagecat_maxrelu_p_kernel(tc, x_words, x_scales, w1, w2, w3, offs
         quantise(w23_codes[:], w23_scale[:], w23_bf[:])
         for u in range(2):
             nc.vector.tensor_tensor(both[:, u], nbr[0][:, u], nbr[1][:, u], MAX)
-        quantise(own_codes[:], own_scale[:], own_bf[:])
+        quantise(own_codes[:, :HALF], own_scale[:, :HALF], own_bf[:, :HALF, :])
         finish(a0, b0)
+        quantise(own_codes[:, HALF:], own_scale[:, HALF:], own_bf[:, HALF:, :])
         finish(a1, b1)
         quantise_top(a0, b0)
         finish(a2, b2)

from contextlib import ExitStack

import concourse.mybir as mybir

K, T, S, V, H, N = 512, 4096, 1024, 512, 512, 128
FLOPS = 2 * K * H * S + 2 * 2 * H * N * V

F32 = mybir.dt.float32
BF16 = mybir.dt.bfloat16
I32 = mybir.dt.int32
U32 = mybir.dt.uint32
U16 = mybir.dt.uint16
U8 = mybir.dt.uint8
FP8X4 = mybir.dt.float8_e4m3fn_x4
MAX = mybir.AluOpType.max
ADD = mybir.AluOpType.add
MULT = mybir.AluOpType.mult
RELU = mybir.ActivationFunctionType.Relu
COPY = mybir.ActivationFunctionType.Copy

P = 128
PACK = 4
BLOCK_ROWS = 8
QUADRANT = 32
PER_COLUMN = 16
BANK = 512
BANKS = 8
HALF = V // 2
CHUNKS = ((0, HALF), (HALF, HALF + P), (HALF + P, V))
HEAD_COLS = 1024
WARM_PASSES, WARM_COLUMNS = 3, 32


def tile_picked_sagecat_maxrelu_p_kernel(tc, x_words, x_scales, w1, w2, w3, offs, cen, pos1, pos2, pos3, out):
    nc = tc.nc
    with ExitStack() as ctx:
        keep = ctx.enter_context(tc.tile_pool(name="keep", bufs=1))
        psum = ctx.enter_context(tc.psum_pool(name="psum", bufs=1))

        def tile(shape, dtype, name, tag=None):
            return keep.tile(shape, dtype, name=name, tag=tag or name, align_bytes=64)

        def quantise(codes, scale, woven):
            nc.vector.quantize_mx(out=codes.bitcast(FP8X4), scales=scale, in_=woven.rearrange("p c j -> p (c j)"))

        def weave_aside(dst, src):
            nc.gpsimd.tensor_scalar(dst, src, 1.0, 0.0, MULT, ADD)

        banks = []

        def next_bank(width, name):
            acc = psum.tile([P, width], F32, name=name, tag="bank%d" % (len(banks) % BANKS))
            banks.append(acc)
            return acc

        offs_sb = keep.tile([P, S // PER_COLUMN], U16, name="offs_sb")
        cen_sb = keep.tile([P, V // PER_COLUMN], U16, name="cen_sb")
        pos_sb = [keep.tile([P, V // PER_COLUMN], U16, name="pos_sb%d" % d) for d in range(3)]
        table_words = tile([P, T], I32, "table_words")
        table_scales = tile([P, T], U8, "table_scales")
        x_scale = tile([P, S], U8, "x_scale")
        w1_raw = tile([P, PACK, H], F32, "w1_raw", "raw")
        words_hbm = x_words[0].rearrange("p c r -> p (c r)").bitcast(I32)
        w1_rows = w1.rearrange("(p j) c -> p j c", j=PACK)
        h = [tile([P, S], F32, "h%d" % t) for t in range(PACK)]

        nc.vector.memset(table_scales[:, : T // 2].bitcast(I32), 0)
        nc.gpsimd.memset(table_scales[:, T // 2 :].bitcast(I32), 0)
        nc.vector.memset(x_scale[:].bitcast(I32), 0)
        nc.sync.dma_start(table_words[:, :HEAD_COLS], words_hbm[:, :HEAD_COLS])
        nc.sync.dma_start(offs_sb[:], offs)
        nc.sync.dma_start(cen_sb[:], cen)
        nc.sync.dma_start(table_scales[0:P:BLOCK_ROWS, :].bitcast(I32), x_scales[0].bitcast(I32))
        nc.sync.dma_start(table_words[:, HEAD_COLS:], words_hbm[:, HEAD_COLS:])
        for e in range(2):
            nc.sync.dma_start(w1_raw[:, 2 * e : 2 * e + 2, :], w1_rows[:, 2 * e : 2 * e + 2, :])
        for dst, pos in zip(pos_sb, (pos1, pos2, pos3)):
            nc.sync.dma_start(dst[:], pos)

        picked_scale = tile([P, S], U8, "picked_scale")
        nc.vector.tensor_copy(picked_scale[:], table_scales[:].indirect(offs_sb[:]))
        for first in range(0, P, QUADRANT):
            nc.sync.dma_start(
                x_scale[first : first + QUADRANT // BLOCK_ROWS, :].bitcast(I32),
                picked_scale[first : first + QUADRANT : BLOCK_ROWS, :].bitcast(I32),
            )
        x_codes = [tile([P, BANK], U32, "x_codes%d" % u) for u in range(S // BANK)]
        for u in range(S // BANK):
            entries = offs_sb[:, u * BANK // PER_COLUMN : (u + 1) * BANK // PER_COLUMN]
            nc.vector.tensor_copy(x_codes[u][:], table_words[:].bitcast(U32).indirect(entries))

        groups = ((0, 1), (1, PACK))
        w1_bf = [tile([P, hi - lo, P, PACK], BF16, "w1_bf%d" % lo) for lo, hi in groups]
        w1_codes = [tile([P, hi - lo, P], U32, "w1_codes%d" % lo, "w1_codes" if lo == 0 else "w1_bf0") for lo, hi in groups]
        w1_scale = tile([P, PACK, P], U8, "w1_scale")

        def round_w1(copy, g, lo, hi, j0, j1):
            first = groups[g][0]
            dst = w1_bf[g][:, lo - first : hi - first, :, j0:j1].rearrange("p t (b r) j -> p t b r j", r=BLOCK_ROWS)
            src = w1_raw[:, j0:j1, :].rearrange("p j (b t r) -> p t b r j", t=PACK, r=BLOCK_ROWS)[:, lo:hi]
            copy(dst, src)

        def round_aside(dst, src):
            nc.gpsimd.tensor_scalar(dst[:, 0], src[:, 0], 1.0, 0.0, MULT, ADD)

        def quantise_w1(g, lo, hi):
            first = groups[g][0]
            quantise(
                w1_codes[g][:, lo - first : hi - first, :].rearrange("p t m -> p (t m)"),
                w1_scale[:, lo:hi, :].rearrange("p t m -> p (t m)"),
                w1_bf[g][:, lo - first : hi - first].rearrange("p t m j -> p (t m) j"),
            )

        def first_product(t, a, b):
            acc = next_bank(b - a, "acc")
            u, c = divmod(a, BANK)
            nc.tensor.matmul_mx(
                out=acc[:],
                lhsT=w1_codes[min(t, 1)][:, max(t - 1, 0), :].bitcast(FP8X4),
                lhsT_scale=w1_scale[:, t, :],
                rhs=x_codes[u][:, c : c + b - a].bitcast(FP8X4),
                rhs_scale=x_scale[:, a:b],
                start=True,
                stop=True,
            )
            return acc

        idle = psum.tile([P, BANK], F32, name="idle", tag="bank%d" % (BANKS - 1))
        for u in range(WARM_PASSES):
            nc.tensor.matmul_mx(
                out=idle[:WARM_COLUMNS, :],
                lhsT=x_codes[0][:, :WARM_COLUMNS].bitcast(FP8X4),
                lhsT_scale=picked_scale[:, :WARM_COLUMNS],
                rhs=x_codes[0][:].bitcast(FP8X4),
                rhs_scale=picked_scale[:, :BANK],
                start=True,
                stop=True,
            )

        round_w1(nc.scalar.copy, 0, 0, 1, 0, 2)
        round_w1(nc.vector.tensor_copy, 0, 0, 1, 2, PACK)
        round_w1(nc.scalar.copy, 1, 1, PACK - 1, 0, 2)
        round_w1(round_aside, 1, PACK - 1, PACK, 0, 2)
        round_w1(nc.vector.tensor_copy, 1, 1, 2, 2, PACK)
        round_w1(nc.scalar.copy, 1, 2, PACK, 2, PACK)
        quantise_w1(0, 0, 1)
        quantise_w1(1, 1, 2)
        quantise_w1(1, 2, PACK)
        narrow = BANK // 2
        stretches = [(0, a, a + narrow) for a in range(0, S, narrow)] + [(1, 0, narrow), (1, narrow, BANK), (1, BANK, S)]
        stretches = stretches + [(t, a, a + BANK) for t in range(2, PACK) for a in range(0, S, BANK)]
        for t, a, b in stretches:
            acc = first_product(t, a, b)
            if b - a == narrow and a % BANK == 0:
                nc.vector.tensor_scalar_max(h[t][:, a:b], acc[:], 0.0)
            else:
                nc.scalar.activation(h[t][:, a:b], acc[:], RELU)

        w23_bf = tile([P, 2 * N, PACK], BF16, "w23_bf")
        w23_scale = tile([P, 2 * N], U8, "w23_scale")
        w23_codes = tile([P, 2 * N], U32, "w23_codes")
        w23_raw = tile([P, PACK, 2 * N], F32, "w23_raw", "raw")
        for e, w in enumerate((w2, w3)):
            for t in range(PACK):
                nc.sync.dma_start(w23_raw[:, t, e * N : (e + 1) * N], w.rearrange("(b t r) c -> t b r c", t=PACK, r=BLOCK_ROWS)[t])
        weave_aside(w23_bf[:], w23_raw[:].rearrange("p j c -> p c j"))

        def fetch_v(dst, idx, t, a=0, b=V):
            nc.vector.tensor_copy(dst, h[t][:].indirect(idx[:, a // PER_COLUMN : b // PER_COLUMN]))

        def fetch_s(dst, idx, t, a=0, b=V):
            nc.scalar.activation(dst, h[t][:].indirect(idx[:, a // PER_COLUMN : b // PER_COLUMN]), COPY)

        own = tile([P, PACK, V], BF16, "own")
        own_bf = tile([P, V, PACK], BF16, "own_bf")
        nbr = [tile([P, 2, V, 2], BF16, "nbr%d" % d) for d in range(3)]
        both = tile([P, 2, V, 2], BF16, "both")
        top_bf = tile([P, V, PACK], BF16, "top_bf")
        own_codes = tile([P, V], U32, "own_codes")
        own_scale = tile([P, V], U8, "own_scale")
        top_codes = tile([P, V], U32, "top_codes")
        top_scale = tile([P, V], U8, "top_scale")

        def fetch_pair(fetch, d, u, a=0, b=V):
            for e in range(2):
                fetch(nbr[d][:, u, a:b, e], pos_sb[d], 2 * u + e, a, b)

        def finish(a, b):
            nc.vector.tensor_tensor(
                top_bf[:, a:b, :].rearrange("p v (u e) -> p v u e", e=2),
                both[:, :, a:b, :].rearrange("p u v e -> p v u e"),
                nbr[2][:, :, a:b, :].rearrange("p u v e -> p v u e"),
                MAX,
            )

        def quantise_top(a, b):
            quantise(top_codes[:, a:b], top_scale[:, a:b], top_bf[:, a:b, :])

        (a0, b0), (a1, b1), (a2, b2) = CHUNKS

        fetch_v(own[:, 0, :], cen_sb, 0)
        fetch_v(nbr[0][:, 0, :, 0], pos_sb[0], 0)
        fetch_v(own[:, 1, :], cen_sb, 1)
        fetch_v(nbr[0][:, 0, :, 1], pos_sb[0], 1)
        for t in range(2, PACK):
            fetch_s(own[:, t, :], cen_sb, t)
        for a in range(0, V, HALF):
            weave_aside(own_bf[:, a : a + HALF, :], own[:, :, a : a + HALF].rearrange("p j c -> p c j"))
        fetch_pair(fetch_v, 1, 0)
        fetch_pair(fetch_v, 2, 0)
        for d in range(2):
            fetch_pair(fetch_s, d, 1)
        for a, b in CHUNKS:
            fetch_pair(fetch_s, 2, 1, a, b)
        quantise(w23_codes[:], w23_scale[:], w23_bf[:])
        for u in range(2):
            nc.vector.tensor_tensor(both[:, u], nbr[0][:, u], nbr[1][:, u], MAX)
        quantise(own_codes[:, :HALF], own_scale[:, :HALF], own_bf[:, :HALF, :])
        finish(a0, b0)
        quantise(own_codes[:, HALF:], own_scale[:, HALF:], own_bf[:, HALF:, :])
        finish(a1, b1)
        quantise_top(a0, b0)
        finish(a2, b2)
        quantise_top(a1, b1)
        quantise_top(a2, b2)

        done = tile([P, V], F32, "done")
        sums = [next_bank(b - a, "sum") for a, b in CHUNKS]
        for e, (codes, scale) in enumerate(((own_codes, own_scale), (top_codes, top_scale))):
            for acc, (a, b) in zip(sums, CHUNKS):
                nc.tensor.matmul_mx(
                    out=acc[:],
                    lhsT=w23_codes[:, e * N : (e + 1) * N].bitcast(FP8X4),
                    lhsT_scale=w23_scale[:, e * N : (e + 1) * N],
                    rhs=codes[:, a:b].bitcast(FP8X4),
                    rhs_scale=scale[:, a:b],
                    start=e == 0,
                    stop=e == 1,
                )
        for acc, (a, b) in zip(sums[:-1], CHUNKS):
            nc.scalar.activation(done[:, a:b], acc[:], RELU)
        nc.vector.tensor_scalar_max(done[:, a2:b2], sums[-1][:], 0.0)
        nc.sync.dma_start(out, done[:])
